import numpy as np, ml_dtypes
CORES = [23,119,17,113]
N = 4
import mx_ref
BF = ml_dtypes.bfloat16
def f(rng, *shape):
    return mx_ref.flush((rng.standard_normal(shape, dtype=np.float32) * np.exp2(rng.integers(-2, 3, shape[:-1] + (1,)))).astype(BF))
def wide(rng, *shape, cols=0):
    v = rng.standard_normal(shape, dtype=np.float32) * np.exp2(rng.integers(-12, 13, shape)).astype(np.float32)
    if cols: v *= np.repeat(np.exp2(rng.integers(-cols, cols + 1, shape[:-2] + (1, shape[-1] // 4))) * (rng.random(shape[:-2] + (1, shape[-1] // 4)) > 0.0625), 4, axis=-1).astype(np.float32)
    return mx_ref.flush(v.astype(BF))
def cols(t, e):
    v = np.concatenate([t.reshape(128, -1, 4), np.zeros((128, 1, 4), BF)], axis=1)
    return np.ascontiguousarray(v[:, e]).reshape(128, -1)
def tile(rs):
    return np.stack(rs, axis=2).reshape(128, -1).astype(BF)
def cut(t, i, w=512):
    return t[:, w * i:w * i + w]
def decode(q):
    o = []
    for b in range(4):
        e = np.zeros((128, 128, 4), np.float32); e[np.arange(128), np.arange(128), b] = 1
        o.append(mx_ref.matmul(mx_ref.quantize(e.reshape(128, 512).astype(BF)), q))
    return np.stack(o, axis=2).reshape(128, -1)
T, CK = 512, 192
def gates(g):
    t = np.zeros((128, 512), BF); t[:, :4 * N] = g
    return np.stack([t] * N)
def plus(g):
    return np.maximum(np.abs(g.astype(np.float32)), np.float32(0.0625)).astype(BF)
def apart(rng):
    g = np.zeros((128, 4 * N), BF)
    for e in range(N): g[8 * e:8 * e + 8, 4 * e:4 * e + 4] = plus(f(rng, 8, 4))
    return g
def setup_inputs(rng):
    return {"x": f(rng, N, 128, 4 * T), "wg": gates(f(rng, 128, 4 * N)), "w1": f(rng, N, 128, 2048)}
def setup_inputs_alike(rng):
    d = setup_inputs(rng); d["wg"] = gates(np.tile(f(rng, 128, 4), (1, N))); return d
def setup_inputs_ties(rng):
    d = setup_inputs(rng); d["wg"] = gates(plus(f(rng, 128, 4 * N))); d["x"] = -plus(d["x"])
    for s in range(N):
        k = rng.permutation(np.arange(T) // 5 if s % 2 else np.arange(T) % (T // (CK + 1)))
        d["x"][s] = d["x"][s].reshape(128, T, 4)[:, k].reshape(128, -1)
    return d
def setup_inputs_split(rng):
    d = setup_inputs(rng); g = apart(rng)
    v = d["x"].astype(np.float32).reshape(N, 128, T, 4)
    for s in range(N):
        p = rng.permutation(T)
        for e in range(N):
            sign = np.full((1, T, 1), -1, np.float32); sign[:, p[(e * CK + np.arange(CK)) % T]] = 1
            v[s, 8 * e:8 * e + 8] = np.abs(v[s, 8 * e:8 * e + 8]) * sign
    d["x"] = v.reshape(N, 128, 4 * T).astype(BF); d["wg"] = gates(g); return d
def setup_inputs_zeros(rng):
    d = setup_inputs(rng); g = apart(rng)
    v = d["x"].astype(np.float32).reshape(N, 128, T, 4)
    for s in range(N):
        for e in range(N):
            p = rng.permutation(T); u = np.abs(v[s, 8 * e:8 * e + 8])
            u[:, p[CK // 2:CK // 2 + CK]] = np.where(rng.random((8, CK, 4)) < 0.5, np.float32(-0.0), np.float32(0.0))
            u[:, p[CK // 2 + CK:]] *= np.float32(-1)
            v[s, 8 * e:8 * e + 8] = u
    d["x"] = v.reshape(N, 128, 4 * T).astype(BF); d["wg"] = gates(g); return d
def setup_inputs_spread(rng):
    d = setup_inputs(rng); d["x"] = wide(rng, N, 128, 4 * T, cols=6); return d
def check_inputs(d):
    b = []
    g = d["wg"].astype(np.float32)
    if (g != g[0]).any() or (g[:, :, 4 * N:] != 0).any(): b.append("wg")
    return b
def reference(x, wg, w1):
    took = []
    for s in range(N):
        z = mx_ref.matmul(mx_ref.quantize(wg[s]), mx_ref.quantize(x[s])) + np.float32(0.0)
        took.append([np.argsort(-z[e], kind="stable")[:CK] for e in range(N)])
    y = np.zeros((N, 128, T, 4), np.float32)
    for e in range(N):
        q = mx_ref.quantize(np.concatenate([cols(x[s], took[s][e]) for s in range(N)], axis=1))
        rs = [np.maximum(mx_ref.matmul(mx_ref.quantize(np.ascontiguousarray(cut(w1[e], i))), q), np.float32(0.0)) * np.float32(0.05) for i in range(4)]
        v = decode(mx_ref.quantize(tile(rs))).reshape(128, N, CK, 4)
        for s in range(N): y[s][:, took[s][e]] += v[:, s]
    return {"y": y.reshape(N, 128, 4 * T)}

@@ -1,0 +1,415 @@
+from concourse.bass import DstId, RemoteDMATransfer
+from concourse.mybir import dt, AluOpType, AxisListType, ActivationFunctionType
+
+A = AluOpType
+F = ActivationFunctionType
+NR, CK, TOK = 4, 192, 512
+NS = 9
+NV = 16 - NS
+CS = 2
+CV = 6 - CS
+PW = 8 + NR * CK
+NCH = 4
+BIG = 1e29
+
+SCRATCH = {
+    "xs": ("sbuf", [128, 2048], "bfloat16"), "ws1": ("sbuf", [128, 2048], "bfloat16"),
+    "gs": ("sbuf", [128, 16], "bfloat16"),
+    "gl1": ("sbuf", [128, 512], "bfloat16"), "gl2": ("sbuf", [128, 512], "bfloat16"),
+    "xq": ("sbuf", [128, 512], "float8_e4m3fn_x4"), "xc": ("sbuf", [128, 512], "uint8"),
+    "wq": ("sbuf", [128, 512], "float8_e4m3fn_x4"), "wc": ("sbuf", [128, 512], "uint8"),
+    "eq": ("sbuf", [128, 512], "float8_e4m3fn_x4"), "ec": ("sbuf", [128, 512], "uint8"),
+    "g1q": ("sbuf", [128, 128], "float8_e4m3fn_x4"), "g1c": ("sbuf", [128, 128], "uint8"),
+    "g2q": ("sbuf", [128, 128], "float8_e4m3fn_x4"), "g2c": ("sbuf", [128, 128], "uint8"),
+    "sq": ("sbuf", [128, 768], "float8_e4m3fn_x4"), "sc": ("sbuf", [128, 768], "uint8"),
+    "rq": ("sbuf", [128, 576], "float8_e4m3fn_x4"), "rc": ("sbuf", [128, 576], "uint8"),
+    "oq": ("sbuf", [128, 768], "float8_e4m3fn_x4"), "oc": ("sbuf", [128, 768], "uint8"),
+    "bq": ("sbuf", [128, 576], "float8_e4m3fn_x4"), "bc": ("sbuf", [128, 576], "uint8"),
+    "ones": ("sbuf", [128, 512], "bfloat16"), "zero": ("sbuf", [128, 512], "bfloat16"),
+    "et": ("sbuf", [128, 2048], "bfloat16"),
+    "ip": ("sbuf", [128, 64], "int32"), "ic": ("sbuf", [128, 64], "int32"), "ie": ("sbuf", [128, 8], "int32"),
+    "pa": ("sbuf", [128, 64], "int32"), "v": ("sbuf", [128, 64], "int32"), "t2": ("sbuf", [128, 32], "int32"),
+    "a1": ("sbuf", [128, 32], "int32"), "l1": ("sbuf", [128, 32], "int32"), "o1": ("sbuf", [128, 32], "uint16"),
+    "a2": ("sbuf", [128, 32], "int32"), "l2": ("sbuf", [128, 32], "int32"), "o2": ("sbuf", [128, 32], "uint16"),
+    "ph": ("sbuf", [128, 8], "int32"), "pr": ("sbuf", [128, 8], "int32"), "pe": ("sbuf", [128, 8], "int32"),
+    "k0": ("sbuf", [128, 8], "int32"), "k1": ("sbuf", [128, 8], "int32"), "k2": ("sbuf", [128, 8], "int32"),
+    "kf": ("sbuf", [128, 8], "float32"), "kh": ("sbuf", [128, 8], "float32"),
+    "base": ("sbuf", [128, 8], "float32"), "m8": ("sbuf", [128, 8], "float32"),
+    "u1": ("sbuf", [128, 32], "int32"), "u2": ("sbuf", [128, 32], "int32"), "u3": ("sbuf", [128, 32], "int32"),
+    "u4": ("sbuf", [128, 32], "int32"), "oT": ("sbuf", [128, 32], "uint16"),
+    "d0": ("sbuf", [128, 36], "float32"), "d1": ("sbuf", [128, 36], "int32"), "d2": ("sbuf", [128, 36], "int32"),
+    "d3": ("sbuf", [128, 36], "int32"), "d4": ("sbuf", [128, 36], "int32"), "oX": ("sbuf", [128, 36], "uint16"),
+    "zT": ("sbuf", [128, 512], "float32"), "junk": ("sbuf", [128, 512 * NS], "bfloat16"),
+    "accS": ("sbuf", [128, NS], "float32"),
+    "cmp": ("sbuf", [128, 512 * NV], "bfloat16"), "scv": ("sbuf", [128, 256 * NV], "bfloat16"),
+    "ma": ("sbuf", [128, 16], "float32"), "mb": ("sbuf", [128, 16], "float32"),
+    "za": ("sbuf", [128, 16], "float32"), "zb": ("sbuf", [128, 16], "float32"),
+    "ex": ("sbuf", [128, 64], "float32"), "exT": ("sbuf", [128, 64], "float32"),
+    "vab": ("sbuf", [128, 2], "float32"), "vbc": ("sbuf", [128, 8], "float32"), "vm": ("sbuf", [128, 8], "float32"),
+    "va": ("sbuf", [128, 1], "float32"), "vb": ("sbuf", [128, 1], "float32"),
+    "gea": ("sbuf", [128, 512], "bfloat16"), "sca": ("sbuf", [128, 256], "bfloat16"),
+    "pen": ("sbuf", [128, 1], "float32"), "tv": ("sbuf", [128, 1], "float32"),
+    "ge": ("sbuf", [128, 512], "bfloat16"), "sgn": ("sbuf", [128, 512], "bfloat16"),
+    "gt": ("sbuf", [128, 512], "bfloat16"), "scg": ("sbuf", [128, 256], "bfloat16"),
+    "dd": ("sbuf", [128, 512], "bfloat16"), "cb": ("sbuf", [128, 528], "bfloat16"),
+    "jk2": ("sbuf", [128, 512 * CS], "bfloat16"), "acc2": ("sbuf", [128, CS], "float32"),
+    "cm2": ("sbuf", [128, 512 * CV], "bfloat16"), "sc2": ("sbuf", [128, 256 * CV], "bfloat16"),
+    "tokc": ("sbuf", [128, 6], "uint16"), "tokw": ("sbuf", [128, 48], "uint16"),
+    "of0": ("sbuf", [128, 48], "uint16"), "of1": ("sbuf", [128, 48], "uint16"),
+    "of2": ("sbuf", [128, 48], "uint16"), "of3": ("sbuf", [128, 48], "uint16"),
+    "h": ("sbuf", [128, 3072], "bfloat16"), "rt": ("sbuf", [128, 3072], "bfloat16"),
+    "cx": ("sbuf", [128, 512], "float32"), "tk": ("sbuf", [128, 512], "bfloat16"),
+    "mf": ("sbuf", [128, 512], "float32"), "mt": ("sbuf", [128, 512], "float32"),
+    "xl": ("sbuf", [128, 576], "float32"), "xp": ("sbuf", [128, 576], "float32"),
+    "wt": ("sbuf", [128, 128], "float32"), "wsl": ("sbuf", [128, 108], "float32"),
+    "lt1": ("sbuf", [128, 64], "float32"), "lt2": ("sbuf", [128, 32], "float32"), "oL": ("sbuf", [128, 32], "uint16"),
+    "sl": ("sbuf", [128, 36], "float32"), "m3": ("sbuf", [128, 12], "float32"), "oS": ("sbuf", [128, 36], "uint16"),
+    "P": ("sbuf", [128, 4 * PW], "float32"), "D": ("sbuf", [128, 4 * 768], "float32"),
+    "ys": ("sbuf", [128, 2048], "float32"),
+}
+for _b in range(8):
+    SCRATCH["ps%d" % _b] = ("psum", [128, 512], "float32")
+SEMAPHORES = ["cv", "cs", "ct", "cg", "lx0", "lx1", "lg", "lw", "wra", "wrb", "lwt", "lws", "sty", "sent",
+              "rd0", "rd1", "rd2", "rd3", "rr0", "rr1", "rr2", "rr3"]
+
+
+def rank_program(g, core, T, topo):
+    me = T.rank_of(core)
+    if me is None:
+        return
+    S = T.sem
+    Q = {"v": g.vector, "s": g.scalar, "t": g.tensor, "g": g, "y": g.sync}
+    cnt, waited, tot = {}, {}, {}
+
+    def need(q, deps):
+        best = {}
+        for sem, val in deps:
+            best[sem] = max(val, best.get(sem, 0))
+        for sem, val in best.items():
+            if waited.get((q, sem), 0) < val:
+                Q[q].wait_ge(S[sem], val)
+                waited[(q, sem)] = val
+
+    def done(q, ins):
+        cnt[q] = cnt.get(q, 0) + 1
+        ins.then_inc(S["c" + q], 1)
+        return ("c" + q, cnt[q])
+
+    def ts(out, in0, s1, op0, s2=None, op1=None, deps=()):
+        need("v", deps)
+        if op1 is None:
+            return done("v", g.vector.tensor_scalar(out, in0, s1, None, op0))
+        return done("v", g.vector.tensor_scalar(out, in0, s1, s2, op0, op1))
+
+    def tt(out, a, b, op, deps=()):
+        need("v", deps)
+        return done("v", g.vector.tensor_tensor(out, a, b, op))
+
+    def cp(out, a, deps=()):
+        need("v", deps)
+        return done("v", g.vector.tensor_copy(out, a))
+
+    def ms(out, c):
+        return done("v", g.vector.memset(out, c))
+
+    def red(out, a, op, deps=()):
+        need("v", deps)
+        return done("v", g.vector.tensor_reduce(out, a, AxisListType.X, op))
+
+    def scan(out, a, b, init, op0, op1, deps=()):
+        need("v", deps)
+        return done("v", g.vector.tensor_tensor_scan(out, a, b, init, op0, op1))
+
+    def tr(out, a, deps=()):
+        need("v", deps)
+        return done("v", g.vector.transpose(out, a))
+
+    def quant(out, sc, a, deps=()):
+        need("v", deps)
+        return done("v", g.vector.quantize_mx(out, sc, a))
+
+    def act(out, a, func, deps=(), **kw):
+        need("s", deps)
+        return done("s", g.scalar.activation(out, a, func, **kw))
+
+    def mm(out, l, ls, r, rs, deps=()):
+        need("t", deps)
+        return done("t", g.tensor.matmul_mx(out, l, ls, r, rs, True, True))
+
+    def dma(q, sem, out, in_, deps=()):
+        need(q, deps)
+        Q[q].dma_start(out, in_).then_inc(S[sem], 16)
+        tot[sem] = tot.get(sem, 0) + 16
+        return (sem, tot[sem])
+
+    def order(r):
+        c = T.cores[r]
+        off = [k for k in range(NR) if topo.chip(T.cores[k]) != topo.chip(c)]
+        on = [k for k in range(NR) if k != r and k not in off]
+        return off + on + [r]
+    O = order(me)
+    OFF, ON = O[:2], O[2]
+    eoff = topo.engines(core, T.cores[OFF[0]])
+    eon = [e for e in topo.engines(core, T.cores[ON]) if e not in eoff] or eoff
+    half = len(eoff) // 2
+    part = {OFF[0]: eoff[:half], OFF[1]: eoff[half:2 * half], ON: eon}
+
+    def mask(es):
+        return sum(1 << e for e in es)
+
+    lg = dma("s", "lg", T.gs[:], T.wg[:, 0:16])
+    lx0 = dma("y", "lx0", T.xs[:, 0:1024], T.x[:, 0:1024])
+    lx1 = dma("y", "lx1", T.xs[:, 1024:2048], T.x[:, 1024:2048])
+
+    need("g", ())
+    ip = done("g", g.iota(T.ip[:], [[0, 64]], 0, 1))
+    ic = done("g", g.iota(T.ic[:], [[16, 64]], 0, 0))
+    ie = done("g", g.iota(T.ie[:], [[1, 4], [0, 2]], 0, 0))
+    on1 = ms(T.ones[:], 1.0)
+    d = ts(T.pa[:], T.ip[:], 15, A.bitwise_and, deps=[ip])
+    v = tt(T.v[:], T.pa[:], T.ic[:], A.add, [d, ic])
+    t2 = ts(T.t2[:], T.v[:, 0:32], 3, A.bitwise_and, deps=[v])
+    a1 = ts(T.a1[:], T.v[:, 0:32], 5, A.arith_shift_right, 12, A.bitwise_and, [v])
+    a2 = ts(T.a2[:], T.v[:, 0:32], 1, A.arith_shift_right, 12, A.bitwise_and, [v])
+    l1 = tt(T.l1[:], T.a1[:], T.t2[:], A.add, [a1, t2])
+    l2 = tt(T.l2[:], T.a2[:], T.t2[:], A.add, [a2, t2])
+    o1 = cp(T.o1[:], T.l1[:], [l1])
+    o2 = cp(T.o2[:], T.l2[:], [l2])
+    zr = ms(T.zero[:], 0.0)
+    exz = ms(T.ex[:], 0.0)
+    cbz = ms(T.cb[:, 0:16], 0.0)
+    for b in range(4):
+        pz = ms(T.P[:, PW * b:PW * b + 8], 0.0)
+    et = []
+    for b in range(4):
+        need("g", [on1])
+        et.append(done("g", g.affine_select(T.et[:, 512 * b:512 * b + 512], T.ones[:], [[1, 512]], A.is_equal, 0.0, -b, -4)))
+
+    g1 = act(T.gl1[:], T.gs[:, 0:16].indirect(T.o1[:, 0:32]), F.Copy, [lg, o1])
+    g2 = cp(T.gl2[:], T.gs[:, 0:16].indirect(T.o2[:, 0:32]), [lg, o2])
+    g1 = quant(T.g1q[:], T.g1c[:], T.gl1[:], [g1])
+    g2 = quant(T.g2q[:], T.g2c[:], T.gl2[:], [g2])
+
+    ph = ts(T.ph[:], T.ip[:, 0:8], 1, A.bitwise_and, deps=[ip])
+    pr = ts(T.pr[:], T.ip[:, 0:8], 3, A.arith_shift_right)
+    pe = ts(T.pe[:], T.ip[:, 0:8], 1, A.arith_shift_right, 3, A.bitwise_and)
+    k0 = ts(T.k0[:], T.ph[:], 96, A.mult, deps=[ph])
+    bs = ts(T.base[:], T.pe[:], 192, A.mult, 7, A.add, [pe])
+    m8 = tt(T.m8[:], T.pe[:], T.ie[:], A.is_equal, [pe, ie])
+    k1 = tt(T.k1[:], T.k0[:], T.pr[:], A.add, [k0, pr])
+    u1 = ts(T.u1[:], T.v[:, 0:32], 31, A.bitwise_and)
+    u2 = ts(T.u2[:], T.v[:, 0:32], 5, A.arith_shift_right)
+    d0 = ts(T.d0[:], T.v[:, 0:36], 1.0 / 36, A.mult, 0.5 / 36 - 0.5, A.add)
+    d3 = ts(T.d3[:], T.v[:, 0:36], 16, A.mult)
+    k2 = tt(T.k2[:], T.k1[:], T.ic[:, 0:8], A.add, [k1])
+    u3 = ts(T.u3[:], T.u1[:], 16, A.mult, deps=[u1])
+    d1 = cp(T.d1[:], T.d0[:], [d0])
+    kf = cp(T.kf[:], T.k2[:], [k2])
+    u4 = tt(T.u4[:], T.u3[:], T.u2[:], A.add, [u3, u2])
+    d2 = ts(T.d2[:], T.d1[:], -575, A.mult, deps=[d1])
+    kh = ts(T.kh[:], T.kf[:], 0.5, A.add, deps=[kf])
+    oT = cp(T.oT[:], T.u4[:], [u4])
+    d4 = tt(T.d4[:], T.d3[:], T.d2[:], A.add, [d3, d2])
+    oX = cp(T.oX[:], T.d4[:], [d4])
+    eqd = quant(T.eq[:], T.ec[:], T.et[:], et)
+
+    x0 = quant(T.xq[:, 0:256], T.xc[:, 0:256], T.xs[:, 0:1024], [lx0])
+    x1 = quant(T.xq[:, 256:512], T.xc[:, 256:512], T.xs[:, 1024:2048], [lx1])
+    lw = dma("y", "lw", T.ws1[:], T.w1[:], [lx0, lx1])
+    zV = mm(T.ps0[:], T.g1q[:], T.g1c[:], T.xq[:], T.xc[:], [g1, x1])
+    zS = mm(T.ps1[:], T.g1q[:], T.g1c[:], T.xq[:], T.xc[:])
+    z2V = mm(T.ps2[:], T.g2q[:], T.g2c[:], T.xq[:], T.xc[:], [g2])
+    z2S = mm(T.ps3[:], T.g2q[:], T.g2c[:], T.xq[:], T.xc[:])
+    zt0 = tr(T.zT[:, 0:256], T.ps0[:, 0:256], [zV])
+    zt1 = tr(T.zT[:, 256:512], T.ps0[:, 256:512])
+    for c in range(NS):
+        aS = act(T.junk[:, 512 * c:512 * c + 512], T.ps1[:], F.Sign, [zS, zt0 if c < 8 else zt1],
+                 bias=T.zT[:, 32 * c:32 * c + 1], scale=-1.0, accum_out=T.accS[:, c:c + 1])
+    prev = None
+    for i in range(NV + 1):
+        if i < NV:
+            c = NS + i
+            cur = ts(T.cmp[:, 512 * i:512 * i + 512], T.ps0[:], T.zT[:, 32 * c:32 * c + 1], A.is_gt, deps=[zt1])
+        if i > 0:
+            k = i - 1
+            wV = scan(T.scv[:, 256 * k:256 * k + 256], T.cmp[:, 512 * k:512 * k + 256], T.cmp[:, 512 * k + 256:512 * k + 512],
+                      -191.5, A.add, A.add, [prev])
+        prev = cur
+    b2 = ts(T.ma[:, NS:16], T.scv[:, 255:256 * NV:256], 0.0, A.is_gt, BIG, A.mult, [wV])
+    b4 = ts(T.mb[:, NS:16], T.scv[:, 255:256 * NV:256], 0.0, A.is_lt, -BIG, A.mult)
+    b1 = ts(T.ma[:, 0:NS], T.accS[:], 128.0, A.is_lt, BIG, A.mult, [aS])
+    b3 = ts(T.mb[:, 0:NS], T.accS[:], 128.0, A.is_ge, -BIG, A.mult)
+    za = tt(T.za[:], T.zT[:, 0:512:32], T.ma[:], A.add, [b1, b2])
+    zb = tt(T.zb[:], T.zT[:, 0:512:32], T.mb[:], A.add, [b3, b4])
+    ra = red(T.ex[:, 0:1], T.za[:], A.min, [za, exz])
+    rb = red(T.ex[:, 32:33], T.zb[:], A.max, [zb])
+    xt = tr(T.exT[:], T.ex[:], [ra, rb])
+    ra = red(T.vab[:, 0:1], T.exT[:, 0:32], A.min, [xt])
+    rb = red(T.vab[:, 1:2], T.exT[:, 32:64], A.max)
+    need("g", [ra, rb])
+    for e in range(NR):
+        bc = done("g", g.partition_broadcast(T.vbc[:, 2 * e:2 * e + 2], T.vab[32 * e:32 * e + 1, :], 128))
+    vm = tt(T.vm[:], T.vbc[:], T.m8[:], A.mult, [bc, m8])
+    va = red(T.va[:], T.vm[:, 0:8:2], A.add, [vm])
+    vb = red(T.vb[:], T.vm[:, 1:8:2], A.add)
+    ga = ts(T.gea[:], T.ps2[:], T.va[:], A.is_ge, deps=[z2V, va])
+    sa = scan(T.sca[:], T.gea[:, 0:256], T.gea[:, 256:512], -191.5, A.add, A.add, [ga])
+    pen = ts(T.pen[:], T.sca[:, 255:256], 0.0, A.is_lt, -9 * BIG, A.mult, [sa])
+    tv = ts(T.tv[:], T.pen[:], T.va[:], A.add, T.vb[:], A.max, [pen, vb])
+    sg = act(T.sgn[:], T.ps3[:], F.Sign, [z2S, tv], bias=T.tv[:], scale=-1.0)
+    ge = ts(T.ge[:], T.ps2[:], T.tv[:], A.is_ge, deps=[tv])
+    gt = ts(T.gt[:], T.sgn[:], 0.0, A.is_lt, -1.0, A.mult, [sg])
+    nd = scan(T.scg[:], T.gt[:, 0:256], T.gt[:, 256:512], 192.0, A.add, A.add, [gt])
+    dd = scan(T.dd[:], T.zero[:], T.gt[:], T.scg[:, 255:256], A.add, A.subtract, [nd, zr])
+    C = scan(T.cb[:, 16:528], T.ge[:], T.dd[:], 0.0, A.add, A.min, [dd, ge])
+    for c in range(CS):
+        aS = act(T.jk2[:, 512 * c:512 * c + 512], T.cb[:, 16:528], F.Sign, [C, kh],
+                 bias=T.kh[:, c:c + 1], scale=-1.0, accum_out=T.acc2[:, c:c + 1])
+    for i in range(CV + 1):
+        if i < CV:
+            cur = ts(T.cm2[:, 512 * i:512 * i + 512], T.cb[:, 16:528], T.kf[:, CS + i:CS + i + 1], A.is_le, deps=[C, kf])
+        if i > 0:
+            k = i - 1
+            wV = scan(T.sc2[:, 256 * k:256 * k + 256], T.cm2[:, 512 * k:512 * k + 256], T.cm2[:, 512 * k + 256:512 * k + 512],
+                      -256.0, A.add, A.add, [prev])
+        prev = cur
+    tc0 = ts(T.tokc[:, 0:CS], T.acc2[:], 0.5, A.mult, 256.0, A.add, [aS])
+    tc1 = ts(T.tokc[:, CS:6], T.sc2[:, 255:256 * CV:256], 256.0, A.add, deps=[wV])
+    for i in range(8):
+        if i % 2:
+            wb = dma("s", "wrb", T.tokw[16 * i:16 * i + 16, :], T.tokc[:], [tc0, tc1])
+        else:
+            wa = dma("y", "wra", T.tokw[16 * i:16 * i + 16, :], T.tokc[:], [tc0, tc1])
+    cx = act(T.cx[:], T.cb[:, 16:528], F.Identity, [C, bs], bias=T.base[:, 0:1])
+    tk = tt(T.tk[:], T.cb[:, 16:528], T.cb[:, 15:527], A.subtract, [C, cbz])
+    mf = tt(T.mf[:], T.cx[:], T.tk[:], A.mult, [cx, tk])
+    wq = quant(T.wq[:], T.wc[:], T.ws1[:], [lw])
+
+    of = [ts(T["of%d" % t][:], T.tokw[:], 4, A.mult, t, A.add, [wa, wb]) for t in (0, 2, 1, 3)]
+    of = {0: of[0], 2: of[1], 1: of[2], 3: of[3]}
+
+    def gather(o):
+        e = O[o]
+        r = []
+        for t in range(4):
+            out = T.h[:, 768 * o + t:768 * o + 768:4]
+            src = T.xs[:, 0:2048].indirect(T["of%d" % t][:, 12 * e:12 * e + 12])
+            r.append(cp(out, src, [of[t]]) if t < 2 else act(out, src, F.Copy, [of[t]]))
+        return r
+
+    def fused(dsts, sb, db, pos_of, sem, code):
+        trs = []
+        for dd_ in dsts:
+            o = O.index(dd_)
+            p = pos_of(dd_)
+            src = T[sb][:, CK * o:CK * o + CK]
+            dst = T[db][:, CK * p:CK * p + CK]
+            if code:
+                src, dst = src.bitcast(dt.uint8), dst.bitcast(dt.uint8)
+            rid, pid, _ = topo.addr(T.cores[dd_])
+            trs.append(RemoteDMATransfer(dst_ids=[DstId(rid=rid, pnc=pid)], dma_engine_mask=mask(part[dd_]),
+                                         remote_sem=S["%s%d" % (sem, me)], srcs=[src], dsts=[dst]))
+            tot["sent"] = tot.get("sent", 0) + len(part[dd_])
+        g.remote_dma_fused(trs, local_sem=S["sent"])
+
+    def place(r):
+        return order(r).index(me)
+
+    def arrived(sem, r):
+        return (sem + str(r), 2 * len(part[r]))
+
+    ga = gather(0) + gather(1)
+    q = quant(T.sq[:, 0:384], T.sc[:, 0:384], T.h[:, 0:1536], ga)
+    need("g", [q])
+    fused(OFF, "sq", "rq", place, "rd", True)
+    fused(OFF, "sc", "rc", place, "rd", False)
+    ga = gather(2)
+    q = quant(T.sq[:, 384:576], T.sc[:, 384:576], T.h[:, 1536:2304], ga)
+    need("g", [q])
+    fused([ON], "sq", "rq", place, "rd", True)
+    fused([ON], "sc", "rc", place, "rd", False)
+    ga = gather(3)
+    qown = quant(T.sq[:, 576:768], T.sc[:, 576:768], T.h[:, 2304:3072], ga)
+
+    free = [[], []]
+    free[0] = [sg, ge]
+
+    def expert(bset, cq, cc, c0, n, o0, deps):
+        rd, outs = [], []
+        m = [mm(T["ps%d" % (4 * bset + i)][:, 0:n], T.wq[:, 128 * i:128 * i + 128], T.wc[:, 128 * i:128 * i + 128],
+                T[cq][:, c0:c0 + n], T[cc][:, c0:c0 + n], list(deps) + [wq] + free[bset]) for i in (0, 2, 1, 3)]
+        m = {0: m[0], 2: m[1], 1: m[2], 3: m[3]}
+        for i in range(4):
+            out = T.rt[:, 768 * o0 + i:768 * o0 + 4 * n:4]
+            src = T["ps%d" % (4 * bset + i)][:, 0:n]
+            if i < 2:
+                rd.append(ts(out, src, 0.0, A.max, 0.05, A.mult, [m[i]]))
+            else:
+                rd.append(act(out, src, F.Relu, [m[i]], scale=0.05))
+        free[bset] = rd
+        return quant(T.oq[:, CK * o0:CK * o0 + n], T.oc[:, CK * o0:CK * o0 + n], T.rt[:, 768 * o0:768 * o0 + 4 * n], rd)
+
+    q3 = expert(1, "sq", "sc", 576, CK, 3, [qown])
+    mt = cp(T.mt[:], T.mf[:].indirect(T.oT[:]), [mf, oT])
+    xl = act(T.xl[:], T.mf[:].indirect(T.tokw[:, 12:48]), F.Copy, [mf, wa, wb])
+    xp = act(T.xp[:], T.xl[:].indirect(T.oX[:]), F.Copy, [xl, oX])
+    for e in range(NR):
+        lt = dma("y", "lwt", T.wt[:, 32 * e:32 * e + 32], T.mt[2 * e:64:8, :], [mt])
+    for e in range(NR - 1):
+        ls = dma("y", "lws", T.wsl[:, 36 * e:36 * e + 36], T.xp[2 * e:64:8, :], [xp])
+    q2 = expert(0, "rq", "rc", 384, CK, 2, [arrived("rd", ON)])
+    need("g", [q2])
+    fused([ON], "oq", "bq", place, "rr", True)
+    fused([ON], "oc", "bc", place, "rr", False)
+    q01 = expert(1, "rq", "rc", 0, 2 * CK, 0, [arrived("rd", r) for r in OFF])
+    need("g", [q01])
+    fused(OFF, "oq", "bq", place, "rr", True)
+    fused(OFF, "oc", "bc", place, "rr", False)
+
+    x = tt(T.lt1[:], T.wt[:, 0:64], T.wt[:, 64:128], A.max, [lt])
+    s0 = cp(T.sl[:, 0:12], T.wsl[:, 0:12], [ls])
+    s1 = tt(T.sl[:, 12:24], T.wsl[:, 12:24], T.wsl[:, 48:60], A.max)
+    s2 = tt(T.m3[:], T.wsl[:, 24:36], T.wsl[:, 60:72], A.max)
+    x = tt(T.lt2[:], T.lt1[:, 0:32], T.lt1[:, 32:64], A.max, [x])
+    s2 = tt(T.sl[:, 24:36], T.m3[:], T.wsl[:, 96:108], A.max, [s2])
+    oL = cp(T.oL[:], T.lt2[:], [x])
+    oS = cp(T.oS[:], T.sl[:], [s0, s1, s2])
+
+    got = {}
+
+    def decode(bset, cq, cc, c0, ranks, deps, split):
+        n = CK * len(ranks)
+        m = [mm(T["ps%d" % (4 * bset + b)][:, 0:n], T.eq[:, 128 * b:128 * b + 128], T.ec[:, 128 * b:128 * b + 128],
+                T[cq][:, c0:c0 + n], T[cc][:, c0:c0 + n], list(deps) + [eqd] + free[bset]) for b in range(4)]
+        free[bset] = []
+        for i, e in enumerate(ranks):
+            for b in range(4):
+                src = T["ps%d" % (4 * bset + b)][:, CK * i:CK * i + CK]
+                out = T.P[:, PW * b + 8:PW * b + 8 + CK] if e == 0 else T.D[:, 768 * e + CK * b:768 * e + CK * b + CK]
+                if split and i == 0 and b % 2 == 0:
+                    got[(e, b)] = cp(out, src, [m[b]])
+                else:
+                    dep = [m[b]] + ([got[(ranks[0], b)]] if i else [])
+                    got[(e, b)] = act(out, src, F.Copy, dep)
+                free[bset].append(got[(e, b)])
+
+    decode(0, "oq", "oc", 576, [me], [q3], False)
+    decode(1, "bq", "bc", 384, [ON], [arrived("rr", ON)], False)
+    decode(0, "bq", "bc", 0, OFF, [arrived("rr", r) for r in OFF], True)
+
+    for e in range(1, NR):
+        for b in range(4):
+            got[(e, b)] = tt(T.P[:, PW * b + 8 + CK * e:PW * b + 8 + CK * (e + 1)],
+                             T.P[:, PW * b:PW * b + 8 + CK * e].indirect(T.oS[:, 12 * (e - 1):12 * e]),
+                             T.D[:, 768 * e + CK * b:768 * e + CK * b + CK], A.add,
+                             [got[(e, b)], got[(e - 1, b)], oS, pz])
+    w, tw = TOK // NCH, 2048 // NCH
+    for ch in range(NCH):
+        r = []
+        for b in range(4):
+            out = T.ys[:, tw * ch + b:tw * ch + tw:4]
+            src = T.P[:, PW * b:PW * b + PW].indirect(T.oL[:, w // 16 * ch:w // 16 * (ch + 1)])
+            dep = [got[(3, b)], oL]
+            r.append(cp(out, src, dep) if b < 2 else act(out, src, F.Copy, dep))
+        st = dma("y", "sty", T.y[:, tw * ch:tw * ch + tw], T.ys[:, tw * ch:tw * ch + tw], r)
+    need("y", [(k, n) for k, n in tot.items()] + [("c" + k, n) for k, n in cnt.items()])

@@ -1,40 +1,38 @@
-from concourse.bass import DstId, RemoteDMATransfer
 from concourse.mybir import dt, AluOpType, AxisListType, ActivationFunctionType
 
 A = AluOpType
 F = ActivationFunctionType
-NR, CK, TOK = 4, 192, 512
+NR, CK = 4, 192
 NS = 9
 NV = 16 - NS
 CS = 2
 CV = 6 - CS
 PW = 8 + NR * CK
-NCH = 4
+XP = ((0, 256), (256, 384), (384, 512))
+YP = ((0, 64), (64, 160), (160, 320), (320, 512))
 BIG = 1e29
 
 SCRATCH = {
-    "xs": ("sbuf", [128, 2048], "bfloat16"), "ws1": ("sbuf", [128, 2048], "bfloat16"),
-    "gs": ("sbuf", [128, 16], "bfloat16"),
-    "gl1": ("sbuf", [128, 512], "bfloat16"), "gl2": ("sbuf", [128, 512], "bfloat16"),
+    "xs": ("sbuf", [128, 2048], "bfloat16"), "xs1": ("sbuf", [128, 2064], "bfloat16"),
+    "xs2": ("sbuf", [128, 2064], "bfloat16"), "xs3": ("sbuf", [128, 2064], "bfloat16"),
+    "ws1": ("sbuf", [128, 2048], "bfloat16"),
+    "gs": ("sbuf", [128, 16], "bfloat16"), "gl1": ("sbuf", [128, 512], "bfloat16"),
     "xq": ("sbuf", [128, 512], "float8_e4m3fn_x4"), "xc": ("sbuf", [128, 512], "uint8"),
     "wq": ("sbuf", [128, 512], "float8_e4m3fn_x4"), "wc": ("sbuf", [128, 512], "uint8"),
     "eq": ("sbuf", [128, 512], "float8_e4m3fn_x4"), "ec": ("sbuf", [128, 512], "uint8"),
     "g1q": ("sbuf", [128, 128], "float8_e4m3fn_x4"), "g1c": ("sbuf", [128, 128], "uint8"),
-    "g2q": ("sbuf", [128, 128], "float8_e4m3fn_x4"), "g2c": ("sbuf", [128, 128], "uint8"),
     "sq": ("sbuf", [128, 768], "float8_e4m3fn_x4"), "sc": ("sbuf", [128, 768], "uint8"),
     "rq": ("sbuf", [128, 576], "float8_e4m3fn_x4"), "rc": ("sbuf", [128, 576], "uint8"),
     "oq": ("sbuf", [128, 768], "float8_e4m3fn_x4"), "oc": ("sbuf", [128, 768], "uint8"),
-    "bq": ("sbuf", [128, 576], "float8_e4m3fn_x4"), "bc": ("sbuf", [128, 576], "uint8"),
+    "bq": ("sbuf", [128, 768], "float8_e4m3fn_x4"), "bc": ("sbuf", [128, 768], "uint8"),
     "ones": ("sbuf", [128, 512], "bfloat16"), "zero": ("sbuf", [128, 512], "bfloat16"),
-    "et": ("sbuf", [128, 2048], "bfloat16"),
-    "ip": ("sbuf", [128, 64], "int32"), "ic": ("sbuf", [128, 64], "int32"), "ie": ("sbuf", [128, 8], "int32"),
+    "zf": ("sbuf", [128, 32], "float32"), "et": ("sbuf", [128, 2048], "bfloat16"),
+    "ip": ("sbuf", [128, 64], "int32"), "ic": ("sbuf", [128, 64], "int32"),
     "pa": ("sbuf", [128, 64], "int32"), "v": ("sbuf", [128, 64], "int32"), "t2": ("sbuf", [128, 32], "int32"),
     "a1": ("sbuf", [128, 32], "int32"), "l1": ("sbuf", [128, 32], "int32"), "o1": ("sbuf", [128, 32], "uint16"),
-    "a2": ("sbuf", [128, 32], "int32"), "l2": ("sbuf", [128, 32], "int32"), "o2": ("sbuf", [128, 32], "uint16"),
     "ph": ("sbuf", [128, 8], "int32"), "pr": ("sbuf", [128, 8], "int32"), "pe": ("sbuf", [128, 8], "int32"),
     "k0": ("sbuf", [128, 8], "int32"), "k1": ("sbuf", [128, 8], "int32"), "k2": ("sbuf", [128, 8], "int32"),
-    "kf": ("sbuf", [128, 8], "float32"), "kh": ("sbuf", [128, 8], "float32"),
-    "base": ("sbuf", [128, 8], "float32"), "m8": ("sbuf", [128, 8], "float32"),
+    "kf": ("sbuf", [128, 8], "float32"), "kh": ("sbuf", [128, 8], "float32"), "base": ("sbuf", [128, 8], "float32"),
     "u1": ("sbuf", [128, 32], "int32"), "u2": ("sbuf", [128, 32], "int32"), "u3": ("sbuf", [128, 32], "int32"),
     "u4": ("sbuf", [128, 32], "int32"), "oT": ("sbuf", [128, 32], "uint16"),
     "d0": ("sbuf", [128, 36], "float32"), "d1": ("sbuf", [128, 36], "int32"), "d2": ("sbuf", [128, 36], "int32"),
@@ -44,19 +42,16 @@ SCRATCH = {
     "cmp": ("sbuf", [128, 512 * NV], "bfloat16"), "scv": ("sbuf", [128, 256 * NV], "bfloat16"),
     "ma": ("sbuf", [128, 16], "float32"), "mb": ("sbuf", [128, 16], "float32"),
     "za": ("sbuf", [128, 16], "float32"), "zb": ("sbuf", [128, 16], "float32"),
+    "ra": ("sbuf", [128, 1], "float32"), "rb": ("sbuf", [128, 1], "float32"),
     "ex": ("sbuf", [128, 64], "float32"), "exT": ("sbuf", [128, 64], "float32"),
-    "vab": ("sbuf", [128, 2], "float32"), "vbc": ("sbuf", [128, 8], "float32"), "vm": ("sbuf", [128, 8], "float32"),
-    "va": ("sbuf", [128, 1], "float32"), "vb": ("sbuf", [128, 1], "float32"),
+    "va": ("sbuf", [128, 1], "float32"), "vb": ("sbuf", [128, 1], "float32"), "n2": ("sbuf", [128, 1], "float32"),
+    "sgA": ("sbuf", [128, 512], "bfloat16"), "sgB": ("sbuf", [128, 512], "bfloat16"),
     "gea": ("sbuf", [128, 512], "bfloat16"), "sca": ("sbuf", [128, 256], "bfloat16"),
-    "pen": ("sbuf", [128, 1], "float32"), "tv": ("sbuf", [128, 1], "float32"),
-    "ge": ("sbuf", [128, 512], "bfloat16"), "sgn": ("sbuf", [128, 512], "bfloat16"),
-    "gt": ("sbuf", [128, 512], "bfloat16"), "scg": ("sbuf", [128, 256], "bfloat16"),
-    "dd": ("sbuf", [128, 512], "bfloat16"), "cb": ("sbuf", [128, 528], "bfloat16"),
+    "gt": ("sbuf", [128, 512], "bfloat16"), "scg": ("sbuf", [128, 256], "bfloat16"), "geb": ("sbuf", [128, 512], "bfloat16"),
+    "dd": ("sbuf", [128, 512], "bfloat16"), "dd2": ("sbuf", [128, 512], "bfloat16"), "cb": ("sbuf", [128, 528], "bfloat16"),
     "jk2": ("sbuf", [128, 512 * CS], "bfloat16"), "acc2": ("sbuf", [128, CS], "float32"),
     "cm2": ("sbuf", [128, 512 * CV], "bfloat16"), "sc2": ("sbuf", [128, 256 * CV], "bfloat16"),
-    "tokc": ("sbuf", [128, 6], "uint16"), "tokw": ("sbuf", [128, 48], "uint16"),
-    "of0": ("sbuf", [128, 48], "uint16"), "of1": ("sbuf", [128, 48], "uint16"),
-    "of2": ("sbuf", [128, 48], "uint16"), "of3": ("sbuf", [128, 48], "uint16"),
+    "tokc": ("sbuf", [128, 6], "uint16"), "tokw": ("sbuf", [128, 48], "uint16"), "tokr": ("sbuf", [128, 48], "uint16"),
     "h": ("sbuf", [128, 3072], "bfloat16"), "rt": ("sbuf", [128, 3072], "bfloat16"),
     "cx": ("sbuf", [128, 512], "float32"), "tk": ("sbuf", [128, 512], "bfloat16"),
     "mf": ("sbuf", [128, 512], "float32"), "mt": ("sbuf", [128, 512], "float32"),
@@ -64,13 +59,13 @@ SCRATCH = {
     "wt": ("sbuf", [128, 128], "float32"), "wsl": ("sbuf", [128, 108], "float32"),
     "lt1": ("sbuf", [128, 64], "float32"), "lt2": ("sbuf", [128, 32], "float32"), "oL": ("sbuf", [128, 32], "uint16"),
     "sl": ("sbuf", [128, 36], "float32"), "m3": ("sbuf", [128, 12], "float32"), "oS": ("sbuf", [128, 36], "uint16"),
-    "P": ("sbuf", [128, 4 * PW], "float32"), "D": ("sbuf", [128, 4 * 768], "float32"),
+    "G": ("sbuf", [128, 2304], "float32"), "P": ("sbuf", [128, 4 * PW], "float32"),
     "ys": ("sbuf", [128, 2048], "float32"),
 }
 for _b in range(8):
     SCRATCH["ps%d" % _b] = ("psum", [128, 512], "float32")
-SEMAPHORES = ["cv", "cs", "ct", "cg", "lx0", "lx1", "lg", "lw", "wra", "wrb", "lwt", "lws", "sty", "sent",
-              "rd0", "rd1", "rd2", "rd3", "rr0", "rr1", "rr2", "rr3"]
+SEMAPHORES = ["cv", "cs", "ct", "cg", "lx0", "lx1", "lx2", "lh1", "lh2", "lh3", "lg", "lw", "wr0", "wr1", "wr2", "wr3",
+              "lwt", "lws", "sty", "sent", "rd0", "rd1", "rd2", "rd3", "rr0", "rr1", "rr2", "rr3"]
 
 
 def rank_program(g, core, T, topo):
@@ -144,39 +139,37 @@ def rank_program(g, core, T, topo):
 
     def order(r):
         c = T.cores[r]
-        off = [k for k in range(NR) if topo.chip(T.cores[k]) != topo.chip(c)]
-        on = [k for k in range(NR) if k != r and k not in off]
-        return off + on + [r]
+        near = [k for k in range(NR) if topo.chip(T.cores[k]) == topo.chip(c)]
+        off = [k for k in range(NR) if k not in near]
+        i = near.index(r)
+        return [off[i], off[1 - i]] + [k for k in near if k != r] + [r]
     O = order(me)
-    OFF, ON = O[:2], O[2]
-    eoff = topo.engines(core, T.cores[OFF[0]])
-    eon = [e for e in topo.engines(core, T.cores[ON]) if e not in eoff] or eoff
-    half = len(eoff) // 2
-    part = {OFF[0]: eoff[:half], OFF[1]: eoff[half:2 * half], ON: eon}
+    eoff = topo.engines(core, T.cores[O[0]])
+    eon = [e for e in topo.engines(core, T.cores[O[2]]) if e not in eoff] or eoff
+    part = {O[0]: eoff, O[1]: eoff, O[2]: eon}
 
     def mask(es):
         return sum(1 << e for e in es)
 
     lg = dma("s", "lg", T.gs[:], T.wg[:, 0:16])
-    lx0 = dma("y", "lx0", T.xs[:, 0:1024], T.x[:, 0:1024])
-    lx1 = dma("y", "lx1", T.xs[:, 1024:2048], T.x[:, 1024:2048])
+    lx = [dma("y", "lx%d" % i, T.xs[:, 4 * a:4 * b], T.x[:, 4 * a:4 * b]) for i, (a, b) in enumerate(XP)]
+    need("y", lx)
+    lsh = {0: lx}
+    for t in (2, 1, 3):
+        lsh[t] = [dma("y", "lh%d" % t, T["xs%d" % t][:, 16 - t:2064 - t], T.x[:])]
+    lw = dma("y", "lw", T.ws1[:], T.w1[:])
 
-    need("g", ())
     ip = done("g", g.iota(T.ip[:], [[0, 64]], 0, 1))
     ic = done("g", g.iota(T.ic[:], [[16, 64]], 0, 0))
-    ie = done("g", g.iota(T.ie[:], [[1, 4], [0, 2]], 0, 0))
     on1 = ms(T.ones[:], 1.0)
     d = ts(T.pa[:], T.ip[:], 15, A.bitwise_and, deps=[ip])
     v = tt(T.v[:], T.pa[:], T.ic[:], A.add, [d, ic])
     t2 = ts(T.t2[:], T.v[:, 0:32], 3, A.bitwise_and, deps=[v])
     a1 = ts(T.a1[:], T.v[:, 0:32], 5, A.arith_shift_right, 12, A.bitwise_and, [v])
-    a2 = ts(T.a2[:], T.v[:, 0:32], 1, A.arith_shift_right, 12, A.bitwise_and, [v])
     l1 = tt(T.l1[:], T.a1[:], T.t2[:], A.add, [a1, t2])
-    l2 = tt(T.l2[:], T.a2[:], T.t2[:], A.add, [a2, t2])
     o1 = cp(T.o1[:], T.l1[:], [l1])
-    o2 = cp(T.o2[:], T.l2[:], [l2])
     zr = ms(T.zero[:], 0.0)
-    exz = ms(T.ex[:], 0.0)
+    zf = ms(T.zf[:], 0.0)
     cbz = ms(T.cb[:, 0:16], 0.0)
     for b in range(4):
         pz = ms(T.P[:, PW * b:PW * b + 8], 0.0)
@@ -186,16 +179,13 @@ def rank_program(g, core, T, topo):
         et.append(done("g", g.affine_select(T.et[:, 512 * b:512 * b + 512], T.ones[:], [[1, 512]], A.is_equal, 0.0, -b, -4)))
 
     g1 = act(T.gl1[:], T.gs[:, 0:16].indirect(T.o1[:, 0:32]), F.Copy, [lg, o1])
-    g2 = cp(T.gl2[:], T.gs[:, 0:16].indirect(T.o2[:, 0:32]), [lg, o2])
     g1 = quant(T.g1q[:], T.g1c[:], T.gl1[:], [g1])
-    g2 = quant(T.g2q[:], T.g2c[:], T.gl2[:], [g2])
 
-    ph = ts(T.ph[:], T.ip[:, 0:8], 1, A.bitwise_and, deps=[ip])
-    pr = ts(T.pr[:], T.ip[:, 0:8], 3, A.arith_shift_right)
-    pe = ts(T.pe[:], T.ip[:, 0:8], 1, A.arith_shift_right, 3, A.bitwise_and)
+    ph = ts(T.ph[:], T.ip[:, 0:8], 1, A.bitwise_and)
+    pr = ts(T.pr[:], T.ip[:, 0:8], 1, A.arith_shift_right, 15, A.bitwise_and)
+    pe = ts(T.pe[:], T.ip[:, 0:8], 5, A.arith_shift_right)
     k0 = ts(T.k0[:], T.ph[:], 96, A.mult, deps=[ph])
     bs = ts(T.base[:], T.pe[:], 192, A.mult, 7, A.add, [pe])
-    m8 = tt(T.m8[:], T.pe[:], T.ie[:], A.is_equal, [pe, ie])
     k1 = tt(T.k1[:], T.k0[:], T.pr[:], A.add, [k0, pr])
     u1 = ts(T.u1[:], T.v[:, 0:32], 31, A.bitwise_and)
     u2 = ts(T.u2[:], T.v[:, 0:32], 5, A.arith_shift_right)
@@ -211,19 +201,15 @@ def rank_program(g, core, T, topo):
     oT = cp(T.oT[:], T.u4[:], [u4])
     d4 = tt(T.d4[:], T.d3[:], T.d2[:], A.add, [d3, d2])
     oX = cp(T.oX[:], T.d4[:], [d4])
-    eqd = quant(T.eq[:], T.ec[:], T.et[:], et)
 
-    x0 = quant(T.xq[:, 0:256], T.xc[:, 0:256], T.xs[:, 0:1024], [lx0])
-    x1 = quant(T.xq[:, 256:512], T.xc[:, 256:512], T.xs[:, 1024:2048], [lx1])
-    lw = dma("y", "lw", T.ws1[:], T.w1[:], [lx0, lx1])
-    zV = mm(T.ps0[:], T.g1q[:], T.g1c[:], T.xq[:], T.xc[:], [g1, x1])
+    xq = [quant(T.xq[:, a:b], T.xc[:, a:b], T.xs[:, 4 * a:4 * b], [lx[i]]) for i, (a, b) in enumerate(XP)]
+    zV = mm(T.ps0[:], T.g1q[:], T.g1c[:], T.xq[:], T.xc[:], [g1] + xq)
     zS = mm(T.ps1[:], T.g1q[:], T.g1c[:], T.xq[:], T.xc[:])
-    z2V = mm(T.ps2[:], T.g2q[:], T.g2c[:], T.xq[:], T.xc[:], [g2])
-    z2S = mm(T.ps3[:], T.g2q[:], T.g2c[:], T.xq[:], T.xc[:])
-    zt0 = tr(T.zT[:, 0:256], T.ps0[:, 0:256], [zV])
-    zt1 = tr(T.zT[:, 256:512], T.ps0[:, 256:512])
+    eqd = quant(T.eq[:], T.ec[:], T.et[:], et)
+    zt0 = tr(T.zT[:, 0:64], T.ps0[:, 0:64], [zV])
+    zt1 = tr(T.zT[:, 64:512], T.ps0[:, 64:512])
     for c in range(NS):
-        aS = act(T.junk[:, 512 * c:512 * c + 512], T.ps1[:], F.Sign, [zS, zt0 if c < 8 else zt1],
+        aS = act(T.junk[:, 512 * c:512 * c + 512], T.ps1[:], F.Sign, [zS, zt0 if c < 2 else zt1],
                  bias=T.zT[:, 32 * c:32 * c + 1], scale=-1.0, accum_out=T.accS[:, c:c + 1])
     prev = None
     for i in range(NV + 1):
@@ -241,27 +227,24 @@ def rank_program(g, core, T, topo):
     b3 = ts(T.mb[:, 0:NS], T.accS[:], 128.0, A.is_ge, -BIG, A.mult)
     za = tt(T.za[:], T.zT[:, 0:512:32], T.ma[:], A.add, [b1, b2])
     zb = tt(T.zb[:], T.zT[:, 0:512:32], T.mb[:], A.add, [b3, b4])
-    ra = red(T.ex[:, 0:1], T.za[:], A.min, [za, exz])
-    rb = red(T.ex[:, 32:33], T.zb[:], A.max, [zb])
-    xt = tr(T.exT[:], T.ex[:], [ra, rb])
-    ra = red(T.vab[:, 0:1], T.exT[:, 0:32], A.min, [xt])
-    rb = red(T.vab[:, 1:2], T.exT[:, 32:64], A.max)
-    need("g", [ra, rb])
-    for e in range(NR):
-        bc = done("g", g.partition_broadcast(T.vbc[:, 2 * e:2 * e + 2], T.vab[32 * e:32 * e + 1, :], 128))
-    vm = tt(T.vm[:], T.vbc[:], T.m8[:], A.mult, [bc, m8])
-    va = red(T.va[:], T.vm[:, 0:8:2], A.add, [vm])
-    vb = red(T.vb[:], T.vm[:, 1:8:2], A.add)
-    ga = ts(T.gea[:], T.ps2[:], T.va[:], A.is_ge, deps=[z2V, va])
-    sa = scan(T.sca[:], T.gea[:, 0:256], T.gea[:, 256:512], -191.5, A.add, A.add, [ga])
-    pen = ts(T.pen[:], T.sca[:, 255:256], 0.0, A.is_lt, -9 * BIG, A.mult, [sa])
-    tv = ts(T.tv[:], T.pen[:], T.va[:], A.add, T.vb[:], A.max, [pen, vb])
-    sg = act(T.sgn[:], T.ps3[:], F.Sign, [z2S, tv], bias=T.tv[:], scale=-1.0)
-    ge = ts(T.ge[:], T.ps2[:], T.tv[:], A.is_ge, deps=[tv])
-    gt = ts(T.gt[:], T.sgn[:], 0.0, A.is_lt, -1.0, A.mult, [sg])
-    nd = scan(T.scg[:], T.gt[:, 0:256], T.gt[:, 256:512], 192.0, A.add, A.add, [gt])
-    dd = scan(T.dd[:], T.zero[:], T.gt[:], T.scg[:, 255:256], A.add, A.subtract, [nd, zr])
-    C = scan(T.cb[:, 16:528], T.ge[:], T.dd[:], 0.0, A.add, A.min, [dd, ge])
+    ra = red(T.ra[:], T.za[:], A.min, [za])
+    rb = red(T.rb[:], T.zb[:], A.max, [zb])
+    xa = ts(T.ex[:, 0:32], T.zf[:], T.ra[:], A.add, deps=[ra, zf])
+    xb = ts(T.ex[:, 32:64], T.zf[:], T.rb[:], A.add, deps=[rb])
+    xt = tr(T.exT[:], T.ex[:], [xa, xb])
+    va = red(T.va[:], T.exT[:, 0:32], A.min, [xt])
+    vb = red(T.vb[:], T.exT[:, 32:64], A.max)
+    sA = act(T.sgA[:], T.ps1[:], F.Sign, [va], bias=T.va[:], scale=-1.0)
+    sB = act(T.sgB[:], T.ps1[:], F.Sign, [vb], bias=T.vb[:], scale=-1.0)
+    ga = ts(T.gea[:], T.ps0[:], T.va[:], A.is_ge, deps=[va])
+    sa = scan(T.sca[:], T.gea[:, 0:256], T.gea[:, 256:512], -192.0, A.add, A.add, [ga])
+    gt = ts(T.gt[:], T.sgA[:], 0.0, A.is_lt, -1.0, A.mult, [sA])
+    n2 = ts(T.n2[:], T.sca[:, 255:256], -1.0, A.mult, 0.0, A.max, [sa])
+    n1 = scan(T.scg[:], T.gt[:, 0:256], T.gt[:, 256:512], 192.0, A.add, A.add, [gt])
+    d1 = scan(T.dd[:], T.zero[:], T.gt[:], T.scg[:, 255:256], A.add, A.subtract, [n1, zr])
+    gb = ts(T.geb[:], T.sgB[:], 0.0, A.is_le, deps=[sB])
+    d2 = scan(T.dd2[:], T.gea[:], T.dd[:], T.n2[:], A.add, A.min, [d1, n2])
+    C = scan(T.cb[:, 16:528], T.geb[:], T.dd2[:], 0.0, A.add, A.min, [d2, gb])
     for c in range(CS):
         aS = act(T.jk2[:, 512 * c:512 * c + 512], T.cb[:, 16:528], F.Sign, [C, kh],
                  bias=T.kh[:, c:c + 1], scale=-1.0, accum_out=T.acc2[:, c:c + 1])
@@ -273,98 +256,79 @@ def rank_program(g, core, T, topo):
             wV = scan(T.sc2[:, 256 * k:256 * k + 256], T.cm2[:, 512 * k:512 * k + 256], T.cm2[:, 512 * k + 256:512 * k + 512],
                       -256.0, A.add, A.add, [prev])
         prev = cur
-    tc0 = ts(T.tokc[:, 0:CS], T.acc2[:], 0.5, A.mult, 256.0, A.add, [aS])
-    tc1 = ts(T.tokc[:, CS:6], T.sc2[:, 255:256 * CV:256], 256.0, A.add, deps=[wV])
-    for i in range(8):
-        if i % 2:
-            wb = dma("s", "wrb", T.tokw[16 * i:16 * i + 16, :], T.tokc[:], [tc0, tc1])
-        else:
-            wa = dma("y", "wra", T.tokw[16 * i:16 * i + 16, :], T.tokc[:], [tc0, tc1])
+    tc0 = ts(T.tokc[:, 0:CS], T.acc2[:], 2.0, A.mult, 1024.0, A.add, [aS])
+    tc1 = ts(T.tokc[:, CS:6], T.sc2[:, 255:256 * CV:256], 4.0, A.mult, 1024.0, A.add, [wV])
+    wr = []
+    for o in range(NR):
+        for i in range(8):
+            w = dma("ys"[i % 2], "wr%d" % o, T.tokw[16 * i:16 * i + 16, 12 * o:12 * o + 12],
+                    T.tokc[32 * O[o]:32 * O[o] + 32, :], [tc0, tc1])
+        wr.append(w)
     cx = act(T.cx[:], T.cb[:, 16:528], F.Identity, [C, bs], bias=T.base[:, 0:1])
-    tk = tt(T.tk[:], T.cb[:, 16:528], T.cb[:, 15:527], A.subtract, [C, cbz])
-    mf = tt(T.mf[:], T.cx[:], T.tk[:], A.mult, [cx, tk])
     wq = quant(T.wq[:], T.wc[:], T.ws1[:], [lw])
-
-    of = [ts(T["of%d" % t][:], T.tokw[:], 4, A.mult, t, A.add, [wa, wb]) for t in (0, 2, 1, 3)]
-    of = {0: of[0], 2: of[1], 1: of[2], 3: of[3]}
+    tk = tt(T.tk[:], T.cb[:, 16:528], T.cb[:, 15:527], A.subtract, [C, cbz])
 
     def gather(o):
-        e = O[o]
         r = []
         for t in range(4):
             out = T.h[:, 768 * o + t:768 * o + 768:4]
-            src = T.xs[:, 0:2048].indirect(T["of%d" % t][:, 12 * e:12 * e + 12])
-            r.append(cp(out, src, [of[t]]) if t < 2 else act(out, src, F.Copy, [of[t]]))
-        return r
+            win = T.xs[:, 0:2048] if t == 0 else T["xs%d" % t][:, 16:2064 - t]
+            src = win.indirect(T.tokw[:, 12 * o:12 * o + 12])
+            dep = [wr[o]] + lsh[t]
+            r.append(cp(out, src, dep) if t < 2 else act(out, src, F.Copy, dep))
+        return quant(T.sq[:, CK * o:CK * o + CK], T.sc[:, CK * o:CK * o + CK], T.h[:, 768 * o:768 * o + 768], r)
 
-    def fused(dsts, sb, db, pos_of, sem, code):
-        trs = []
-        for dd_ in dsts:
-            o = O.index(dd_)
-            p = pos_of(dd_)
-            src = T[sb][:, CK * o:CK * o + CK]
-            dst = T[db][:, CK * p:CK * p + CK]
+    def send(o, sb, sp, db, dp, sem, dep):
+        r = O[o]
+        p = order(r).index(me)
+        rid, pid, _ = topo.addr(T.cores[r])
+        need("g", [dep])
+        for a, b, code in ((sb, db, True), (sp, dp, False)):
+            src, dst = T[a][:, CK * o:CK * o + CK], T[b][:, CK * p:CK * p + CK]
             if code:
                 src, dst = src.bitcast(dt.uint8), dst.bitcast(dt.uint8)
-            rid, pid, _ = topo.addr(T.cores[dd_])
-            trs.append(RemoteDMATransfer(dst_ids=[DstId(rid=rid, pnc=pid)], dma_engine_mask=mask(part[dd_]),
-                                         remote_sem=S["%s%d" % (sem, me)], srcs=[src], dsts=[dst]))
-            tot["sent"] = tot.get("sent", 0) + len(part[dd_])
-        g.remote_dma_fused(trs, local_sem=S["sent"])
+            g.remote_dma(out_ap=dst, in_ap=src, remote_sem=S["%s%d" % (sem, me)], local_sem=S["sent"], pid=pid,
+                         routing_id=rid, dma_engine_mask=mask(part[r]))
+            tot["sent"] = tot.get("sent", 0) + len(part[r])
 
-    def place(r):
-        return order(r).index(me)
+    def arrived(sem, o):
+        return (sem + str(O[o]), 2 * len(part[O[o]]))
 
-    def arrived(sem, r):
-        return (sem + str(r), 2 * len(part[r]))
+    for o in range(3):
+        send(o, "sq", "sc", "rq", "rc", "rd", gather(o))
+    qown = gather(3)
+    mf = tt(T.mf[:], T.cx[:], T.tk[:], A.mult, [cx, tk])
+    tr4 = ts(T.tokr[:], T.tokw[:], 0.25, A.mult, deps=wr)
 
-    ga = gather(0) + gather(1)
-    q = quant(T.sq[:, 0:384], T.sc[:, 0:384], T.h[:, 0:1536], ga)
-    need("g", [q])
-    fused(OFF, "sq", "rq", place, "rd", True)
-    fused(OFF, "sc", "rc", place, "rd", False)
-    ga = gather(2)
-    q = quant(T.sq[:, 384:576], T.sc[:, 384:576], T.h[:, 1536:2304], ga)
-    need("g", [q])
-    fused([ON], "sq", "rq", place, "rd", True)
-    fused([ON], "sc", "rc", place, "rd", False)
-    ga = gather(3)
-    qown = quant(T.sq[:, 576:768], T.sc[:, 576:768], T.h[:, 2304:3072], ga)
+    free = [[sA, sB, C], []]
 
-    free = [[], []]
-    free[0] = [sg, ge]
-
-    def expert(bset, cq, cc, c0, n, o0, deps):
-        rd, outs = [], []
-        m = [mm(T["ps%d" % (4 * bset + i)][:, 0:n], T.wq[:, 128 * i:128 * i + 128], T.wc[:, 128 * i:128 * i + 128],
-                T[cq][:, c0:c0 + n], T[cc][:, c0:c0 + n], list(deps) + [wq] + free[bset]) for i in (0, 2, 1, 3)]
-        m = {0: m[0], 2: m[1], 1: m[2], 3: m[3]}
+    def expert(bset, cq, cc, o, qout, qsc, deps):
+        rd, m = [], {}
+        for i in (0, 2, 1, 3):
+            m[i] = mm(T["ps%d" % (4 * bset + i)][:, 0:CK], T.wq[:, 128 * i:128 * i + 128], T.wc[:, 128 * i:128 * i + 128],
+                      T[cq][:, CK * o:CK * o + CK], T[cc][:, CK * o:CK * o + CK], list(deps) + [wq] + free[bset])
         for i in range(4):
-            out = T.rt[:, 768 * o0 + i:768 * o0 + 4 * n:4]
-            src = T["ps%d" % (4 * bset + i)][:, 0:n]
+            out = T.rt[:, 768 * o + i:768 * o + 768:4]
+            src = T["ps%d" % (4 * bset + i)][:, 0:CK]
             if i < 2:
                 rd.append(ts(out, src, 0.0, A.max, 0.05, A.mult, [m[i]]))
             else:
                 rd.append(act(out, src, F.Relu, [m[i]], scale=0.05))
         free[bset] = rd
-        return quant(T.oq[:, CK * o0:CK * o0 + n], T.oc[:, CK * o0:CK * o0 + n], T.rt[:, 768 * o0:768 * o0 + 4 * n], rd)
+        return quant(T[qout][:, CK * o:CK * o + CK], T[qsc][:, CK * o:CK * o + CK], T.rt[:, 768 * o:768 * o + 768], rd)
 
-    q3 = expert(1, "sq", "sc", 576, CK, 3, [qown])
+    q3 = expert(1, "sq", "sc", 3, "bq", "bc", [qown])
     mt = cp(T.mt[:], T.mf[:].indirect(T.oT[:]), [mf, oT])
-    xl = act(T.xl[:], T.mf[:].indirect(T.tokw[:, 12:48]), F.Copy, [mf, wa, wb])
+    for e in range(1, NR):
+        c0 = 12 * O.index(e)
+        xl = act(T.xl[:, CK * (e - 1):CK * e], T.mf[:].indirect(T.tokr[:, c0:c0 + 12]), F.Copy, [mf, tr4])
     xp = act(T.xp[:], T.xl[:].indirect(T.oX[:]), F.Copy, [xl, oX])
     for e in range(NR):
-        lt = dma("y", "lwt", T.wt[:, 32 * e:32 * e + 32], T.mt[2 * e:64:8, :], [mt])
+        lt = dma("y", "lwt", T.wt[:, 32 * e:32 * e + 32], T.mt[32 * e:32 * e + 8, :], [mt])
     for e in range(NR - 1):
-        ls = dma("y", "lws", T.wsl[:, 36 * e:36 * e + 36], T.xp[2 * e:64:8, :], [xp])
-    q2 = expert(0, "rq", "rc", 384, CK, 2, [arrived("rd", ON)])
-    need("g", [q2])
-    fused([ON], "oq", "bq", place, "rr", True)
-    fused([ON], "oc", "bc", place, "rr", False)
-    q01 = expert(1, "rq", "rc", 0, 2 * CK, 0, [arrived("rd", r) for r in OFF])
-    need("g", [q01])
-    fused(OFF, "oq", "bq", place, "rr", True)
-    fused(OFF, "oc", "bc", place, "rr", False)
+        ls = dma("y", "lws", T.wsl[:, 36 * e:36 * e + 36], T.xp[32 * e:32 * e + 8, :], [xp])
+    for bset, o in ((0, 0), (1, 2), (0, 1)):
+        send(o, "oq", "oc", "bq", "bc", "rr", expert(bset, "rq", "rc", o, "oq", "oc", [arrived("rd", o)]))
 
     x = tt(T.lt1[:], T.wt[:, 0:64], T.wt[:, 64:128], A.max, [lt])
     s0 = cp(T.sl[:, 0:12], T.wsl[:, 0:12], [ls])
@@ -375,41 +339,53 @@ def rank_program(g, core, T, topo):
     oL = cp(T.oL[:], T.lt2[:], [x])
     oS = cp(T.oS[:], T.sl[:], [s0, s1, s2])
 
-    got = {}
-
-    def decode(bset, cq, cc, c0, ranks, deps, split):
-        n = CK * len(ranks)
-        m = [mm(T["ps%d" % (4 * bset + b)][:, 0:n], T.eq[:, 128 * b:128 * b + 128], T.ec[:, 128 * b:128 * b + 128],
-                T[cq][:, c0:c0 + n], T[cc][:, c0:c0 + n], list(deps) + [eqd] + free[bset]) for b in range(4)]
-        free[bset] = []
-        for i, e in enumerate(ranks):
-            for b in range(4):
-                src = T["ps%d" % (4 * bset + b)][:, CK * i:CK * i + CK]
-                out = T.P[:, PW * b + 8:PW * b + 8 + CK] if e == 0 else T.D[:, 768 * e + CK * b:768 * e + CK * b + CK]
-                if split and i == 0 and b % 2 == 0:
-                    got[(e, b)] = cp(out, src, [m[b]])
-                else:
-                    dep = [m[b]] + ([got[(ranks[0], b)]] if i else [])
-                    got[(e, b)] = act(out, src, F.Copy, dep)
-                free[bset].append(got[(e, b)])
-
-    decode(0, "oq", "oc", 576, [me], [q3], False)
-    decode(1, "bq", "bc", 384, [ON], [arrived("rr", ON)], False)
-    decode(0, "bq", "bc", 0, OFF, [arrived("rr", r) for r in OFF], True)
-
-    for e in range(1, NR):
+    dm = {}
+    for bset, o, deps in ((1, 2, [arrived("rr", 2), q3]), (0, 0, [arrived("rr", 0), arrived("rr", 1)])):
         for b in range(4):
-            got[(e, b)] = tt(T.P[:, PW * b + 8 + CK * e:PW * b + 8 + CK * (e + 1)],
-                             T.P[:, PW * b:PW * b + 8 + CK * e].indirect(T.oS[:, 12 * (e - 1):12 * e]),
-                             T.D[:, 768 * e + CK * b:768 * e + CK * b + CK], A.add,
-                             [got[(e, b)], got[(e - 1, b)], oS, pz])
-    w, tw = TOK // NCH, 2048 // NCH
-    for ch in range(NCH):
+            m = mm(T["ps%d" % (4 * bset + b)][:, 0:2 * CK], T.eq[:, 128 * b:128 * b + 128], T.ec[:, 128 * b:128 * b + 128],
+                   T.bq[:, CK * o:CK * o + 2 * CK], T.bc[:, CK * o:CK * o + 2 * CK], deps + [eqd] + free[bset])
+            for i in range(2):
+                dm[(O[o + i], b)] = (m, T["ps%d" % (4 * bset + b)][:, CK * i:CK * i + CK])
+
+    got, gs = {}, {}
+
+    def first(b, vec):
+        m, src = dm[(0, b)]
+        out = T.P[:, PW * b + 8:PW * b + 8 + CK]
+        got[b] = cp(out, src, [m]) if vec else act(out, src, F.Copy, [m])
+
+    def pick(e, b):
+        out = T.G[:, 768 * (e - 1) + CK * b:768 * (e - 1) + CK * b + CK]
+        src = T.P[:, PW * b:PW * b + 8 + CK * e].indirect(T.oS[:, 12 * (e - 1):12 * e])
+        dep = [got[b], oS, pz]
+        gs[b] = (cp(out, src, dep) if b == 0 else act(out, src, F.Copy, dep), out)
+
+    def add(e, b):
+        m, src = dm[(e, b)]
+        got[b] = tt(T.P[:, PW * b + 8 + CK * e:PW * b + 8 + CK * (e + 1)], src, gs[b][1], A.add, [m, gs[b][0], got[b]])
+
+    if O.index(0) < 2:
+        first(0, True), first(1, False), pick(1, 0), pick(1, 1), add(1, 0)
+        first(2, True), pick(1, 2), add(1, 1)
+        first(3, True), pick(1, 3), add(1, 2), add(1, 3)
+    else:
+        for b in range(4):
+            first(b, b % 2 == 0)
+        for b in range(4):
+            pick(1, b)
+        for b in range(4):
+            add(1, b)
+    for e in range(2, NR):
+        for b in range(4):
+            pick(e, b)
+        for b in range(4):
+            add(e, b)
+    for a, z in YP:
         r = []
         for b in range(4):
-            out = T.ys[:, tw * ch + b:tw * ch + tw:4]
-            src = T.P[:, PW * b:PW * b + PW].indirect(T.oL[:, w // 16 * ch:w // 16 * (ch + 1)])
-            dep = [got[(3, b)], oL]
+            out = T.ys[:, 4 * a + b:4 * z:4]
+            src = T.P[:, PW * b:PW * b + PW].indirect(T.oL[:, a // 16:z // 16])
+            dep = [got[b], oL]
             r.append(cp(out, src, dep) if b < 2 else act(out, src, F.Copy, dep))
-        st = dma("y", "sty", T.y[:, tw * ch:tw * ch + tw], T.ys[:, tw * ch:tw * ch + tw], r)
+        st = dma("y", "sty", T.y[:, 4 * a:4 * z], T.ys[:, 4 * a:4 * z], r)
     need("y", [(k, n) for k, n in tot.items()] + [("c" + k, n) for k, n in cnt.items()])

@@ -30,6 +30,7 @@ SCRATCH = {
     "ip": ("sbuf", [128, 64], "int32"), "ic": ("sbuf", [128, 64], "int32"),
     "pa": ("sbuf", [128, 64], "int32"), "v": ("sbuf", [128, 64], "int32"), "t2": ("sbuf", [128, 32], "int32"),
     "a1": ("sbuf", [128, 32], "int32"), "l1": ("sbuf", [128, 32], "int32"), "o1": ("sbuf", [128, 32], "uint16"),
+    "a2": ("sbuf", [128, 32], "int32"), "a3": ("sbuf", [128, 32], "int32"), "a4": ("sbuf", [128, 32], "int32"),
     "ph": ("sbuf", [128, 8], "int32"), "pr": ("sbuf", [128, 8], "int32"), "pe": ("sbuf", [128, 8], "int32"),
     "k0": ("sbuf", [128, 8], "int32"), "k1": ("sbuf", [128, 8], "int32"), "k2": ("sbuf", [128, 8], "int32"),
     "kf": ("sbuf", [128, 8], "float32"), "kh": ("sbuf", [128, 8], "float32"), "base": ("sbuf", [128, 8], "float32"),
@@ -144,6 +145,9 @@ def rank_program(g, core, T, topo):
         i = near.index(r)
         return [off[i], off[1 - i]] + [k for k in near if k != r] + [r]
     O = order(me)
+    SLOT = (0, 3, 2, 1)
+    E = [1, 0, 2, 3] if 1 in O[2:] else [0, 1, 2, 3]
+    B = [E.index(r) for r in O]
     eoff = topo.engines(core, T.cores[O[0]])
     eon = [e for e in topo.engines(core, T.cores[O[2]]) if e not in eoff] or eoff
     part = {O[0]: eoff, O[1]: eoff, O[2]: eon}
@@ -166,6 +170,11 @@ def rank_program(g, core, T, topo):
     v = tt(T.v[:], T.pa[:], T.ic[:], A.add, [d, ic])
     t2 = ts(T.t2[:], T.v[:, 0:32], 3, A.bitwise_and, deps=[v])
     a1 = ts(T.a1[:], T.v[:, 0:32], 5, A.arith_shift_right, 12, A.bitwise_and, [v])
+    if E[0] == 1:
+        a2 = ts(T.a2[:], T.a1[:], 8, A.is_lt, deps=[a1])
+        a3 = ts(T.a3[:], T.a1[:], -2, A.mult, 4, A.add, [a1])
+        a4 = tt(T.a4[:], T.a2[:], T.a3[:], A.mult, [a2, a3])
+        a1 = tt(T.a1[:], T.a1[:], T.a4[:], A.add, [a4])
     l1 = tt(T.l1[:], T.a1[:], T.t2[:], A.add, [a1, t2])
     o1 = cp(T.o1[:], T.l1[:], [l1])
     zr = ms(T.zero[:], 0.0)
@@ -177,9 +186,6 @@ def rank_program(g, core, T, topo):
     for b in range(4):
         need("g", [on1])
         et.append(done("g", g.affine_select(T.et[:, 512 * b:512 * b + 512], T.ones[:], [[1, 512]], A.is_equal, 0.0, -b, -4)))
-
-    g1 = act(T.gl1[:], T.gs[:, 0:16].indirect(T.o1[:, 0:32]), F.Copy, [lg, o1])
-    g1 = quant(T.g1q[:], T.g1c[:], T.gl1[:], [g1])
 
     ph = ts(T.ph[:], T.ip[:, 0:8], 1, A.bitwise_and)
     pr = ts(T.pr[:], T.ip[:, 0:8], 1, A.arith_shift_right, 15, A.bitwise_and)
@@ -202,10 +208,12 @@ def rank_program(g, core, T, topo):
     d4 = tt(T.d4[:], T.d3[:], T.d2[:], A.add, [d3, d2])
     oX = cp(T.oX[:], T.d4[:], [d4])
 
+    g1 = act(T.gl1[:], T.gs[:, 0:16].indirect(T.o1[:, 0:32]), F.Copy, [lg, o1])
+    g1 = quant(T.g1q[:], T.g1c[:], T.gl1[:], [g1])
+
     xq = [quant(T.xq[:, a:b], T.xc[:, a:b], T.xs[:, 4 * a:4 * b], [lx[i]]) for i, (a, b) in enumerate(XP)]
     zV = mm(T.ps0[:], T.g1q[:], T.g1c[:], T.xq[:], T.xc[:], [g1] + xq)
     zS = mm(T.ps1[:], T.g1q[:], T.g1c[:], T.xq[:], T.xc[:])
-    eqd = quant(T.eq[:], T.ec[:], T.et[:], et)
     zt0 = tr(T.zT[:, 0:64], T.ps0[:, 0:64], [zV])
     zt1 = tr(T.zT[:, 64:512], T.ps0[:, 64:512])
     for c in range(NS):
@@ -262,7 +270,7 @@ def rank_program(g, core, T, topo):
     for o in range(NR):
         for i in range(8):
             w = dma("ys"[i % 2], "wr%d" % o, T.tokw[16 * i:16 * i + 16, 12 * o:12 * o + 12],
-                    T.tokc[32 * O[o]:32 * O[o] + 32, :], [tc0, tc1])
+                    T.tokc[32 * B[o]:32 * B[o] + 32, :], [tc0, tc1])
         wr.append(w)
     cx = act(T.cx[:], T.cb[:, 16:528], F.Identity, [C, bs], bias=T.base[:, 0:1])
     wq = quant(T.wq[:], T.wc[:], T.ws1[:], [lw])
@@ -281,6 +289,8 @@ def rank_program(g, core, T, topo):
     def send(o, sb, sp, db, dp, sem, dep):
         r = O[o]
         p = order(r).index(me)
+        if sem == "rr":
+            p = SLOT[p]
         rid, pid, _ = topo.addr(T.cores[r])
         need("g", [dep])
         for a, b, code in ((sb, db, True), (sp, dp, False)):
@@ -302,7 +312,7 @@ def rank_program(g, core, T, topo):
 
     free = [[sA, sB, C], []]
 
-    def expert(bset, cq, cc, o, qout, qsc, deps):
+    def expert(bset, cq, cc, o, qout, qsc, z, deps):
         rd, m = [], {}
         for i in (0, 2, 1, 3):
             m[i] = mm(T["ps%d" % (4 * bset + i)][:, 0:CK], T.wq[:, 128 * i:128 * i + 128], T.wc[:, 128 * i:128 * i + 128],
@@ -315,20 +325,21 @@ def rank_program(g, core, T, topo):
             else:
                 rd.append(act(out, src, F.Relu, [m[i]], scale=0.05))
         free[bset] = rd
-        return quant(T[qout][:, CK * o:CK * o + CK], T[qsc][:, CK * o:CK * o + CK], T.rt[:, 768 * o:768 * o + 768], rd)
+        return quant(T[qout][:, CK * z:CK * z + CK], T[qsc][:, CK * z:CK * z + CK], T.rt[:, 768 * o:768 * o + 768], rd)
 
-    q3 = expert(1, "sq", "sc", 3, "bq", "bc", [qown])
+    q3 = expert(1, "sq", "sc", 3, "bq", "bc", SLOT[3], [qown])
+    eqd = quant(T.eq[:], T.ec[:], T.et[:], et)
     mt = cp(T.mt[:], T.mf[:].indirect(T.oT[:]), [mf, oT])
-    for e in range(1, NR):
-        c0 = 12 * O.index(e)
-        xl = act(T.xl[:, CK * (e - 1):CK * e], T.mf[:].indirect(T.tokr[:, c0:c0 + 12]), F.Copy, [mf, tr4])
+    for q in range(1, NR):
+        c0 = 12 * B.index(q)
+        xl = act(T.xl[:, CK * (q - 1):CK * q], T.mf[:].indirect(T.tokr[:, c0:c0 + 12]), F.Copy, [mf, tr4])
     xp = act(T.xp[:], T.xl[:].indirect(T.oX[:]), F.Copy, [xl, oX])
-    for e in range(NR):
-        lt = dma("y", "lwt", T.wt[:, 32 * e:32 * e + 32], T.mt[32 * e:32 * e + 8, :], [mt])
-    for e in range(NR - 1):
-        ls = dma("y", "lws", T.wsl[:, 36 * e:36 * e + 36], T.xp[32 * e:32 * e + 8, :], [xp])
+    for q in range(NR):
+        lt = dma("y", "lwt", T.wt[:, 32 * q:32 * q + 32], T.mt[32 * q:32 * q + 8, :], [mt])
+    for q in range(NR - 1):
+        ls = dma("y", "lws", T.wsl[:, 36 * q:36 * q + 36], T.xp[32 * q:32 * q + 8, :], [xp])
     for bset, o in ((0, 0), (1, 2), (0, 1)):
-        send(o, "oq", "oc", "bq", "bc", "rr", expert(bset, "rq", "rc", o, "oq", "oc", [arrived("rd", o)]))
+        send(o, "oq", "oc", "bq", "bc", "rr", expert(bset, "rq", "rc", o, "oq", "oc", o, [arrived("rd", o)]))
 
     x = tt(T.lt1[:], T.wt[:, 0:64], T.wt[:, 64:128], A.max, [lt])
     s0 = cp(T.sl[:, 0:12], T.wsl[:, 0:12], [ls])
@@ -339,47 +350,46 @@ def rank_program(g, core, T, topo):
     oL = cp(T.oL[:], T.lt2[:], [x])
     oS = cp(T.oS[:], T.sl[:], [s0, s1, s2])
 
-    dm = {}
-    for bset, o, deps in ((1, 2, [arrived("rr", 2), q3]), (0, 0, [arrived("rr", 0), arrived("rr", 1)])):
+    dm, got, gs = {}, {}, {}
+
+    def decode(bset, z, blocks, deps):
+        n = len(blocks) * CK
         for b in range(4):
-            m = mm(T["ps%d" % (4 * bset + b)][:, 0:2 * CK], T.eq[:, 128 * b:128 * b + 128], T.ec[:, 128 * b:128 * b + 128],
-                   T.bq[:, CK * o:CK * o + 2 * CK], T.bc[:, CK * o:CK * o + 2 * CK], deps + [eqd] + free[bset])
-            for i in range(2):
-                dm[(O[o + i], b)] = (m, T["ps%d" % (4 * bset + b)][:, CK * i:CK * i + CK])
+            m = mm(T["ps%d" % (4 * bset + b)][:, 0:n], T.eq[:, 128 * b:128 * b + 128], T.ec[:, 128 * b:128 * b + 128],
+                   T.bq[:, CK * z:CK * z + n], T.bc[:, CK * z:CK * z + n], deps[b] + [eqd])
+            for i, q in enumerate(blocks):
+                dm[(q, b)] = (m, T["ps%d" % (4 * bset + b)][:, CK * i:CK * i + CK])
 
-    got, gs = {}, {}
+    own = B[3] == 0
+    decode(0, 0, [B[0], B[3]] if own else [B[0]], [[arrived("rr", 0), q3] + free[0]] * 4)
+    decode(1, 2, [B[2]], [[arrived("rr", 2)] + free[1]] * 4)
 
-    def first(b, vec):
+    def first(b):
         m, src = dm[(0, b)]
         out = T.P[:, PW * b + 8:PW * b + 8 + CK]
-        got[b] = cp(out, src, [m]) if vec else act(out, src, F.Copy, [m])
+        got[b] = cp(out, src, [m]) if b % 2 == 0 else act(out, src, F.Copy, [m])
 
-    def pick(e, b):
-        out = T.G[:, 768 * (e - 1) + CK * b:768 * (e - 1) + CK * b + CK]
-        src = T.P[:, PW * b:PW * b + 8 + CK * e].indirect(T.oS[:, 12 * (e - 1):12 * e])
+    def pick(q, b):
+        out = T.G[:, 768 * (q - 1) + CK * b:768 * (q - 1) + CK * b + CK]
+        src = T.P[:, PW * b:PW * b + 8 + CK * q].indirect(T.oS[:, 12 * (q - 1):12 * q])
         dep = [got[b], oS, pz]
         gs[b] = (cp(out, src, dep) if b == 0 else act(out, src, F.Copy, dep), out)
 
-    def add(e, b):
-        m, src = dm[(e, b)]
-        got[b] = tt(T.P[:, PW * b + 8 + CK * e:PW * b + 8 + CK * (e + 1)], src, gs[b][1], A.add, [m, gs[b][0], got[b]])
+    def add(q, b):
+        m, src = dm[(q, b)]
+        got[b] = tt(T.P[:, PW * b + 8 + CK * q:PW * b + 8 + CK * (q + 1)], src, gs[b][1], A.add, [m, gs[b][0], got[b]])
 
-    if O.index(0) < 2:
-        first(0, True), first(1, False), pick(1, 0), pick(1, 1), add(1, 0)
-        first(2, True), pick(1, 2), add(1, 1)
-        first(3, True), pick(1, 3), add(1, 2), add(1, 3)
-    else:
+    for b in range(4):
+        first(b)
+    for q in range(1, NR):
+        if q == (2 if own else 1):
+            decode(0 if own else 1, 3, [B[1]], [[arrived("rr", 1), got[b]] for b in range(4)])
+        if q == B[3]:
+            decode(0 if B[0] == q - 1 else 1, 1, [q], [[got[b]] for b in range(4)])
         for b in range(4):
-            first(b, b % 2 == 0)
+            pick(q, b)
         for b in range(4):
-            pick(1, b)
-        for b in range(4):
-            add(1, b)
-    for e in range(2, NR):
-        for b in range(4):
-            pick(e, b)
-        for b in range(4):
-            add(e, b)
+            add(q, b)
     for a, z in YP:
         r = []
         for b in range(4):

from concourse.mybir import dt, AluOpType, AxisListType, ActivationFunctionType

A = AluOpType
F = ActivationFunctionType
NR, CK = 4, 192
NS = 9
NV = 16 - NS
CS = 2
CV = 6 - CS
PW = 8 + NR * CK
XP = ((0, 256), (256, 384), (384, 512))
YP = ((0, 64), (64, 160), (160, 320), (320, 512))
BIG = 1e29

SCRATCH = {
    "xs": ("sbuf", [128, 2048], "bfloat16"), "xs1": ("sbuf", [128, 2064], "bfloat16"),
    "xs2": ("sbuf", [128, 2064], "bfloat16"), "xs3": ("sbuf", [128, 2064], "bfloat16"),
    "ws1": ("sbuf", [128, 2048], "bfloat16"),
    "gs": ("sbuf", [128, 16], "bfloat16"), "gl1": ("sbuf", [128, 512], "bfloat16"),
    "xq": ("sbuf", [128, 512], "float8_e4m3fn_x4"), "xc": ("sbuf", [128, 512], "uint8"),
    "wq": ("sbuf", [128, 512], "float8_e4m3fn_x4"), "wc": ("sbuf", [128, 512], "uint8"),
    "eq": ("sbuf", [128, 512], "float8_e4m3fn_x4"), "ec": ("sbuf", [128, 512], "uint8"),
    "g1q": ("sbuf", [128, 128], "float8_e4m3fn_x4"), "g1c": ("sbuf", [128, 128], "uint8"),
    "sq": ("sbuf", [128, 768], "float8_e4m3fn_x4"), "sc": ("sbuf", [128, 768], "uint8"),
    "rq": ("sbuf", [128, 576], "float8_e4m3fn_x4"), "rc": ("sbuf", [128, 576], "uint8"),
    "oq": ("sbuf", [128, 768], "float8_e4m3fn_x4"), "oc": ("sbuf", [128, 768], "uint8"),
    "bq": ("sbuf", [128, 768], "float8_e4m3fn_x4"), "bc": ("sbuf", [128, 768], "uint8"),
    "ones": ("sbuf", [128, 512], "bfloat16"), "zero": ("sbuf", [128, 512], "bfloat16"),
    "zf": ("sbuf", [128, 32], "float32"), "et": ("sbuf", [128, 2048], "bfloat16"),
    "ip": ("sbuf", [128, 64], "int32"), "ic": ("sbuf", [128, 64], "int32"),
    "pa": ("sbuf", [128, 64], "int32"), "v": ("sbuf", [128, 64], "int32"), "t2": ("sbuf", [128, 32], "int32"),
    "a1": ("sbuf", [128, 32], "int32"), "l1": ("sbuf", [128, 32], "int32"), "o1": ("sbuf", [128, 32], "uint16"),
    "a2": ("sbuf", [128, 32], "int32"), "a3": ("sbuf", [128, 32], "int32"), "a4": ("sbuf", [128, 32], "int32"),
    "ph": ("sbuf", [128, 8], "int32"), "pr": ("sbuf", [128, 8], "int32"), "pe": ("sbuf", [128, 8], "int32"),
    "k0": ("sbuf", [128, 8], "int32"), "k1": ("sbuf", [128, 8], "int32"), "k2": ("sbuf", [128, 8], "int32"),
    "kf": ("sbuf", [128, 8], "float32"), "kh": ("sbuf", [128, 8], "float32"), "base": ("sbuf", [128, 8], "float32"),
    "u1": ("sbuf", [128, 32], "int32"), "u2": ("sbuf", [128, 32], "int32"), "u3": ("sbuf", [128, 32], "int32"),
    "u4": ("sbuf", [128, 32], "int32"), "oT": ("sbuf", [128, 32], "uint16"),
    "d0": ("sbuf", [128, 36], "float32"), "d1": ("sbuf", [128, 36], "int32"), "d2": ("sbuf", [128, 36], "int32"),
    "d3": ("sbuf", [128, 36], "int32"), "d4": ("sbuf", [128, 36], "int32"), "oX": ("sbuf", [128, 36], "uint16"),
    "zT": ("sbuf", [128, 512], "float32"), "junk": ("sbuf", [128, 512 * NS], "bfloat16"),
    "accS": ("sbuf", [128, NS], "float32"),
    "cmp": ("sbuf", [128, 512 * NV], "bfloat16"), "scv": ("sbuf", [128, 256 * NV], "bfloat16"),
    "ma": ("sbuf", [128, 16], "float32"), "mb": ("sbuf", [128, 16], "float32"),
    "za": ("sbuf", [128, 16], "float32"), "zb": ("sbuf", [128, 16], "float32"),
    "ra": ("sbuf", [128, 1], "float32"), "rb": ("sbuf", [128, 1], "float32"),
    "ex": ("sbuf", [128, 64], "float32"), "exT": ("sbuf", [128, 64], "float32"),
    "va": ("sbuf", [128, 1], "float32"), "vb": ("sbuf", [128, 1], "float32"), "n2": ("sbuf", [128, 1], "float32"),
    "sgA": ("sbuf", [128, 512], "bfloat16"), "sgB": ("sbuf", [128, 512], "bfloat16"),
    "gea": ("sbuf", [128, 512], "bfloat16"), "sca": ("sbuf", [128, 256], "bfloat16"),
    "gt": ("sbuf", [128, 512], "bfloat16"), "scg": ("sbuf", [128, 256], "bfloat16"), "geb": ("sbuf", [128, 512], "bfloat16"),
    "dd": ("sbuf", [128, 512], "bfloat16"), "dd2": ("sbuf", [128, 512], "bfloat16"), "cb": ("sbuf", [128, 528], "bfloat16"),
    "jk2": ("sbuf", [128, 512 * CS], "bfloat16"), "acc2": ("sbuf", [128, CS], "float32"),
    "cm2": ("sbuf", [128, 512 * CV], "bfloat16"), "sc2": ("sbuf", [128, 256 * CV], "bfloat16"),
    "tokc": ("sbuf", [128, 6], "uint16"), "tokw": ("sbuf", [128, 48], "uint16"), "tokr": ("sbuf", [128, 48], "uint16"),
    "h": ("sbuf", [128, 3072], "bfloat16"), "rt": ("sbuf", [128, 3072], "bfloat16"),
    "cx": ("sbuf", [128, 512], "float32"), "tk": ("sbuf", [128, 512], "bfloat16"),
    "mf": ("sbuf", [128, 512], "float32"), "mt": ("sbuf", [128, 512], "float32"),
    "xl": ("sbuf", [128, 576], "float32"), "xp": ("sbuf", [128, 576], "float32"),
    "wt": ("sbuf", [128, 128], "float32"), "wsl": ("sbuf", [128, 108], "float32"),
    "lt1": ("sbuf", [128, 64], "float32"), "lt2": ("sbuf", [128, 32], "float32"), "oL": ("sbuf", [128, 32], "uint16"),
    "sl": ("sbuf", [128, 36], "float32"), "m3": ("sbuf", [128, 12], "float32"), "oS": ("sbuf", [128, 36], "uint16"),
    "G": ("sbuf", [128, 2304], "float32"), "P": ("sbuf", [128, 4 * PW], "float32"),
    "ys": ("sbuf", [128, 2048], "float32"),
}
for _b in range(8):
    SCRATCH["ps%d" % _b] = ("psum", [128, 512], "float32")
SEMAPHORES = ["cv", "cs", "ct", "cg", "lx0", "lx1", "lx2", "lh1", "lh2", "lh3", "lg", "lw", "wr0", "wr1", "wr2", "wr3",
              "lwt", "lws", "sty", "sent", "rd0", "rd1", "rd2", "rd3", "rr0", "rr1", "rr2", "rr3"]


def rank_program(g, core, T, topo):
    me = T.rank_of(core)
    if me is None:
        return
    S = T.sem
    Q = {"v": g.vector, "s": g.scalar, "t": g.tensor, "g": g, "y": g.sync}
    cnt, waited, tot = {}, {}, {}

    def need(q, deps):
        best = {}
        for sem, val in deps:
            best[sem] = max(val, best.get(sem, 0))
        for sem, val in best.items():
            if waited.get((q, sem), 0) < val:
                Q[q].wait_ge(S[sem], val)
                waited[(q, sem)] = val

    def done(q, ins):
        cnt[q] = cnt.get(q, 0) + 1
        ins.then_inc(S["c" + q], 1)
        return ("c" + q, cnt[q])

    def ts(out, in0, s1, op0, s2=None, op1=None, deps=()):
        need("v", deps)
        if op1 is None:
            return done("v", g.vector.tensor_scalar(out, in0, s1, None, op0))
        return done("v", g.vector.tensor_scalar(out, in0, s1, s2, op0, op1))

    def tt(out, a, b, op, deps=()):
        need("v", deps)
        return done("v", g.vector.tensor_tensor(out, a, b, op))

    def cp(out, a, deps=()):
        need("v", deps)
        return done("v", g.vector.tensor_copy(out, a))

    def ms(out, c):
        return done("v", g.vector.memset(out, c))

    def red(out, a, op, deps=()):
        need("v", deps)
        return done("v", g.vector.tensor_reduce(out, a, AxisListType.X, op))

    def scan(out, a, b, init, op0, op1, deps=()):
        need("v", deps)
        return done("v", g.vector.tensor_tensor_scan(out, a, b, init, op0, op1))

    def tr(out, a, deps=()):
        need("v", deps)
        return done("v", g.vector.transpose(out, a))

    def quant(out, sc, a, deps=()):
        need("v", deps)
        return done("v", g.vector.quantize_mx(out, sc, a))

    def act(out, a, func, deps=(), **kw):
        need("s", deps)
        return done("s", g.scalar.activation(out, a, func, **kw))

    def mm(out, l, ls, r, rs, deps=()):
        need("t", deps)
        return done("t", g.tensor.matmul_mx(out, l, ls, r, rs, True, True))

    def dma(q, sem, out, in_, deps=()):
        need(q, deps)
        Q[q].dma_start(out, in_).then_inc(S[sem], 16)
        tot[sem] = tot.get(sem, 0) + 16
        return (sem, tot[sem])

    def order(r):
        c = T.cores[r]
        near = [k for k in range(NR) if topo.chip(T.cores[k]) == topo.chip(c)]
        off = [k for k in range(NR) if k not in near]
        i = near.index(r)
        return [off[i], off[1 - i]] + [k for k in near if k != r] + [r]
    O = order(me)
    SLOT = (0, 3, 2, 1)
    E = [1, 0, 2, 3] if 1 in O[2:] else [0, 1, 2, 3]
    B = [E.index(r) for r in O]
    eoff = topo.engines(core, T.cores[O[0]])
    eon = [e for e in topo.engines(core, T.cores[O[2]]) if e not in eoff] or eoff
    part = {O[0]: eoff, O[1]: eoff, O[2]: eon}

    def mask(es):
        return sum(1 << e for e in es)

    lg = dma("s", "lg", T.gs[:], T.wg[:, 0:16])
    lx = [dma("y", "lx%d" % i, T.xs[:, 4 * a:4 * b], T.x[:, 4 * a:4 * b]) for i, (a, b) in enumerate(XP)]
    need("y", lx)
    lsh = {0: lx}
    for t in (2, 1, 3):
        lsh[t] = [dma("y", "lh%d" % t, T["xs%d" % t][:, 16 - t:2064 - t], T.x[:])]
    lw = dma("y", "lw", T.ws1[:], T.w1[:])

    ip = done("g", g.iota(T.ip[:], [[0, 64]], 0, 1))
    ic = done("g", g.iota(T.ic[:], [[16, 64]], 0, 0))
    on1 = ms(T.ones[:], 1.0)
    d = ts(T.pa[:], T.ip[:], 15, A.bitwise_and, deps=[ip])
    v = tt(T.v[:], T.pa[:], T.ic[:], A.add, [d, ic])
    t2 = ts(T.t2[:], T.v[:, 0:32], 3, A.bitwise_and, deps=[v])
    a1 = ts(T.a1[:], T.v[:, 0:32], 5, A.arith_shift_right, 12, A.bitwise_and, [v])
    if E[0] == 1:
        a2 = ts(T.a2[:], T.a1[:], 8, A.is_lt, deps=[a1])
        a3 = ts(T.a3[:], T.a1[:], -2, A.mult, 4, A.add, [a1])
        a4 = tt(T.a4[:], T.a2[:], T.a3[:], A.mult, [a2, a3])
        a1 = tt(T.a1[:], T.a1[:], T.a4[:], A.add, [a4])
    l1 = tt(T.l1[:], T.a1[:], T.t2[:], A.add, [a1, t2])
    o1 = cp(T.o1[:], T.l1[:], [l1])
    zr = ms(T.zero[:], 0.0)
    zf = ms(T.zf[:], 0.0)
    cbz = ms(T.cb[:, 0:16], 0.0)
    for b in range(4):
        pz = ms(T.P[:, PW * b:PW * b + 8], 0.0)
    et = []
    for b in range(4):
        need("g", [on1])
        et.append(done("g", g.affine_select(T.et[:, 512 * b:512 * b + 512], T.ones[:], [[1, 512]], A.is_equal, 0.0, -b, -4)))

    ph = ts(T.ph[:], T.ip[:, 0:8], 1, A.bitwise_and)
    pr = ts(T.pr[:], T.ip[:, 0:8], 1, A.arith_shift_right, 15, A.bitwise_and)
    pe = ts(T.pe[:], T.ip[:, 0:8], 5, A.arith_shift_right)
    k0 = ts(T.k0[:], T.ph[:], 96, A.mult, deps=[ph])
    bs = ts(T.base[:], T.pe[:], 192, A.mult, 7, A.add, [pe])
    k1 = tt(T.k1[:], T.k0[:], T.pr[:], A.add, [k0, pr])
    u1 = ts(T.u1[:], T.v[:, 0:32], 31, A.bitwise_and)
    u2 = ts(T.u2[:], T.v[:, 0:32], 5, A.arith_shift_right)
    d0 = ts(T.d0[:], T.v[:, 0:36], 1.0 / 36, A.mult, 0.5 / 36 - 0.5, A.add)
    d3 = ts(T.d3[:], T.v[:, 0:36], 16, A.mult)
    k2 = tt(T.k2[:], T.k1[:], T.ic[:, 0:8], A.add, [k1])
    u3 = ts(T.u3[:], T.u1[:], 16, A.mult, deps=[u1])
    d1 = cp(T.d1[:], T.d0[:], [d0])
    kf = cp(T.kf[:], T.k2[:], [k2])
    u4 = tt(T.u4[:], T.u3[:], T.u2[:], A.add, [u3, u2])
    d2 = ts(T.d2[:], T.d1[:], -575, A.mult, deps=[d1])
    kh = ts(T.kh[:], T.kf[:], 0.5, A.add, deps=[kf])
    oT = cp(T.oT[:], T.u4[:], [u4])
    d4 = tt(T.d4[:], T.d3[:], T.d2[:], A.add, [d3, d2])
    oX = cp(T.oX[:], T.d4[:], [d4])

    g1 = act(T.gl1[:], T.gs[:, 0:16].indirect(T.o1[:, 0:32]), F.Copy, [lg, o1])
    g1 = quant(T.g1q[:], T.g1c[:], T.gl1[:], [g1])

    xq = [quant(T.xq[:, a:b], T.xc[:, a:b], T.xs[:, 4 * a:4 * b], [lx[i]]) for i, (a, b) in enumerate(XP)]
    zV = mm(T.ps0[:], T.g1q[:], T.g1c[:], T.xq[:], T.xc[:], [g1] + xq)
    zS = mm(T.ps1[:], T.g1q[:], T.g1c[:], T.xq[:], T.xc[:])
    zt0 = tr(T.zT[:, 0:64], T.ps0[:, 0:64], [zV])
    zt1 = tr(T.zT[:, 64:512], T.ps0[:, 64:512])
    for c in range(NS):
        aS = act(T.junk[:, 512 * c:512 * c + 512], T.ps1[:], F.Sign, [zS, zt0 if c < 2 else zt1],
                 bias=T.zT[:, 32 * c:32 * c + 1], scale=-1.0, accum_out=T.accS[:, c:c + 1])
    prev = None
    for i in range(NV + 1):
        if i < NV:
            c = NS + i
            cur = ts(T.cmp[:, 512 * i:512 * i + 512], T.ps0[:], T.zT[:, 32 * c:32 * c + 1], A.is_gt, deps=[zt1])
        if i > 0:
            k = i - 1
            wV = scan(T.scv[:, 256 * k:256 * k + 256], T.cmp[:, 512 * k:512 * k + 256], T.cmp[:, 512 * k + 256:512 * k + 512],
                      -191.5, A.add, A.add, [prev])
        prev = cur
    b2 = ts(T.ma[:, NS:16], T.scv[:, 255:256 * NV:256], 0.0, A.is_gt, BIG, A.mult, [wV])
    b4 = ts(T.mb[:, NS:16], T.scv[:, 255:256 * NV:256], 0.0, A.is_lt, -BIG, A.mult)
    b1 = ts(T.ma[:, 0:NS], T.accS[:], 128.0, A.is_lt, BIG, A.mult, [aS])
    b3 = ts(T.mb[:, 0:NS], T.accS[:], 128.0, A.is_ge, -BIG, A.mult)
    za = tt(T.za[:], T.zT[:, 0:512:32], T.ma[:], A.add, [b1, b2])
    zb = tt(T.zb[:], T.zT[:, 0:512:32], T.mb[:], A.add, [b3, b4])
    ra = red(T.ra[:], T.za[:], A.min, [za])
    rb = red(T.rb[:], T.zb[:], A.max, [zb])
    xa = ts(T.ex[:, 0:32], T.zf[:], T.ra[:], A.add, deps=[ra, zf])
    xb = ts(T.ex[:, 32:64], T.zf[:], T.rb[:], A.add, deps=[rb])
    xt = tr(T.exT[:], T.ex[:], [xa, xb])
    va = red(T.va[:], T.exT[:, 0:32], A.min, [xt])
    vb = red(T.vb[:], T.exT[:, 32:64], A.max)
    sA = act(T.sgA[:], T.ps1[:], F.Sign, [va], bias=T.va[:], scale=-1.0)
    sB = act(T.sgB[:], T.ps1[:], F.Sign, [vb], bias=T.vb[:], scale=-1.0)
    ga = ts(T.gea[:], T.ps0[:], T.va[:], A.is_ge, deps=[va])
    sa = scan(T.sca[:], T.gea[:, 0:256], T.gea[:, 256:512], -192.0, A.add, A.add, [ga])
    gt = ts(T.gt[:], T.sgA[:], 0.0, A.is_lt, -1.0, A.mult, [sA])
    n2 = ts(T.n2[:], T.sca[:, 255:256], -1.0, A.mult, 0.0, A.max, [sa])
    n1 = scan(T.scg[:], T.gt[:, 0:256], T.gt[:, 256:512], 192.0, A.add, A.add, [gt])
    d1 = scan(T.dd[:], T.zero[:], T.gt[:], T.scg[:, 255:256], A.add, A.subtract, [n1, zr])
    gb = ts(T.geb[:], T.sgB[:], 0.0, A.is_le, deps=[sB])
    d2 = scan(T.dd2[:], T.gea[:], T.dd[:], T.n2[:], A.add, A.min, [d1, n2])
    C = scan(T.cb[:, 16:528], T.geb[:], T.dd2[:], 0.0, A.add, A.min, [d2, gb])
    for c in range(CS):
        aS = act(T.jk2[:, 512 * c:512 * c + 512], T.cb[:, 16:528], F.Sign, [C, kh],
                 bias=T.kh[:, c:c + 1], scale=-1.0, accum_out=T.acc2[:, c:c + 1])
    for i in range(CV + 1):
        if i < CV:
            cur = ts(T.cm2[:, 512 * i:512 * i + 512], T.cb[:, 16:528], T.kf[:, CS + i:CS + i + 1], A.is_le, deps=[C, kf])
        if i > 0:
            k = i - 1
            wV = scan(T.sc2[:, 256 * k:256 * k + 256], T.cm2[:, 512 * k:512 * k + 256], T.cm2[:, 512 * k + 256:512 * k + 512],
                      -256.0, A.add, A.add, [prev])
        prev = cur
    tc0 = ts(T.tokc[:, 0:CS], T.acc2[:], 2.0, A.mult, 1024.0, A.add, [aS])
    tc1 = ts(T.tokc[:, CS:6], T.sc2[:, 255:256 * CV:256], 4.0, A.mult, 1024.0, A.add, [wV])
    wr = []
    for o in range(NR):
        for i in range(8):
            w = dma("ys"[i % 2], "wr%d" % o, T.tokw[16 * i:16 * i + 16, 12 * o:12 * o + 12],
                    T.tokc[32 * B[o]:32 * B[o] + 32, :], [tc0, tc1])
        wr.append(w)
    cx = act(T.cx[:], T.cb[:, 16:528], F.Identity, [C, bs], bias=T.base[:, 0:1])
    wq = quant(T.wq[:], T.wc[:], T.ws1[:], [lw])
    tk = tt(T.tk[:], T.cb[:, 16:528], T.cb[:, 15:527], A.subtract, [C, cbz])

    def gather(o):
        r = []
        for t in range(4):
            out = T.h[:, 768 * o + t:768 * o + 768:4]
            win = T.xs[:, 0:2048] if t == 0 else T["xs%d" % t][:, 16:2064 - t]
            src = win.indirect(T.tokw[:, 12 * o:12 * o + 12])
            dep = [wr[o]] + lsh[t]
            r.append(cp(out, src, dep) if t < 2 else act(out, src, F.Copy, dep))
        return quant(T.sq[:, CK * o:CK * o + CK], T.sc[:, CK * o:CK * o + CK], T.h[:, 768 * o:768 * o + 768], r)

    def send(o, sb, sp, db, dp, sem, dep):
        r = O[o]
        p = order(r).index(me)
        if sem == "rr":
            p = SLOT[p]
        rid, pid, _ = topo.addr(T.cores[r])
        need("g", [dep])
        for a, b, code in ((sb, db, True), (sp, dp, False)):
            src, dst = T[a][:, CK * o:CK * o + CK], T[b][:, CK * p:CK * p + CK]
            if code:
                src, dst = src.bitcast(dt.uint8), dst.bitcast(dt.uint8)
            g.remote_dma(out_ap=dst, in_ap=src, remote_sem=S["%s%d" % (sem, me)], local_sem=S["sent"], pid=pid,
                         routing_id=rid, dma_engine_mask=mask(part[r]))
            tot["sent"] = tot.get("sent", 0) + len(part[r])

    def arrived(sem, o):
        return (sem + str(O[o]), 2 * len(part[O[o]]))

    for o in range(3):
        send(o, "sq", "sc", "rq", "rc", "rd", gather(o))
    qown = gather(3)
    mf = tt(T.mf[:], T.cx[:], T.tk[:], A.mult, [cx, tk])
    tr4 = ts(T.tokr[:], T.tokw[:], 0.25, A.mult, deps=wr)

    free = [[sA, sB, C], []]

    def expert(bset, cq, cc, o, qout, qsc, z, deps):
        rd, m = [], {}
        for i in (0, 2, 1, 3):
            m[i] = mm(T["ps%d" % (4 * bset + i)][:, 0:CK], T.wq[:, 128 * i:128 * i + 128], T.wc[:, 128 * i:128 * i + 128],
                      T[cq][:, CK * o:CK * o + CK], T[cc][:, CK * o:CK * o + CK], list(deps) + [wq] + free[bset])
        for i in range(4):
            out = T.rt[:, 768 * o + i:768 * o + 768:4]
            src = T["ps%d" % (4 * bset + i)][:, 0:CK]
            if i < 2:
                rd.append(ts(out, src, 0.0, A.max, 0.05, A.mult, [m[i]]))
            else:
                rd.append(act(out, src, F.Relu, [m[i]], scale=0.05))
        free[bset] = rd
        return quant(T[qout][:, CK * z:CK * z + CK], T[qsc][:, CK * z:CK * z + CK], T.rt[:, 768 * o:768 * o + 768], rd)

    q3 = expert(1, "sq", "sc", 3, "bq", "bc", SLOT[3], [qown])
    eqd = quant(T.eq[:], T.ec[:], T.et[:], et)
    mt = cp(T.mt[:], T.mf[:].indirect(T.oT[:]), [mf, oT])
    for q in range(1, NR):
        c0 = 12 * B.index(q)
        xl = act(T.xl[:, CK * (q - 1):CK * q], T.mf[:].indirect(T.tokr[:, c0:c0 + 12]), F.Copy, [mf, tr4])
    xp = act(T.xp[:], T.xl[:].indirect(T.oX[:]), F.Copy, [xl, oX])
    for q in range(NR):
        lt = dma("y", "lwt", T.wt[:, 32 * q:32 * q + 32], T.mt[32 * q:32 * q + 8, :], [mt])
    for q in range(NR - 1):
        ls = dma("y", "lws", T.wsl[:, 36 * q:36 * q + 36], T.xp[32 * q:32 * q + 8, :], [xp])
    for bset, o in ((0, 0), (1, 2), (0, 1)):
        send(o, "oq", "oc", "bq", "bc", "rr", expert(bset, "rq", "rc", o, "oq", "oc", o, [arrived("rd", o)]))

    x = tt(T.lt1[:], T.wt[:, 0:64], T.wt[:, 64:128], A.max, [lt])
    s0 = cp(T.sl[:, 0:12], T.wsl[:, 0:12], [ls])
    s1 = tt(T.sl[:, 12:24], T.wsl[:, 12:24], T.wsl[:, 48:60], A.max)
    s2 = tt(T.m3[:], T.wsl[:, 24:36], T.wsl[:, 60:72], A.max)
    x = tt(T.lt2[:], T.lt1[:, 0:32], T.lt1[:, 32:64], A.max, [x])
    s2 = tt(T.sl[:, 24:36], T.m3[:], T.wsl[:, 96:108], A.max, [s2])
    oL = cp(T.oL[:], T.lt2[:], [x])
    oS = cp(T.oS[:], T.sl[:], [s0, s1, s2])

    dm, got, gs = {}, {}, {}

    def decode(bset, z, blocks, deps):
        n = len(blocks) * CK
        for b in range(4):
            m = mm(T["ps%d" % (4 * bset + b)][:, 0:n], T.eq[:, 128 * b:128 * b + 128], T.ec[:, 128 * b:128 * b + 128],
                   T.bq[:, CK * z:CK * z + n], T.bc[:, CK * z:CK * z + n], deps[b] + [eqd])
            for i, q in enumerate(blocks):
                dm[(q, b)] = (m, T["ps%d" % (4 * bset + b)][:, CK * i:CK * i + CK])

    own = B[3] == 0
    decode(0, 0, [B[0], B[3]] if own else [B[0]], [[arrived("rr", 0), q3] + free[0]] * 4)
    decode(1, 2, [B[2]], [[arrived("rr", 2)] + free[1]] * 4)

    def first(b):
        m, src = dm[(0, b)]
        out = T.P[:, PW * b + 8:PW * b + 8 + CK]
        got[b] = cp(out, src, [m]) if b % 2 == 0 else act(out, src, F.Copy, [m])

    def pick(q, b):
        out = T.G[:, 768 * (q - 1) + CK * b:768 * (q - 1) + CK * b + CK]
        src = T.P[:, PW * b:PW * b + 8 + CK * q].indirect(T.oS[:, 12 * (q - 1):12 * q])
        dep = [got[b], oS, pz]
        gs[b] = (cp(out, src, dep) if b == 0 else act(out, src, F.Copy, dep), out)

    def add(q, b):
        m, src = dm[(q, b)]
        got[b] = tt(T.P[:, PW * b + 8 + CK * q:PW * b + 8 + CK * (q + 1)], src, gs[b][1], A.add, [m, gs[b][0], got[b]])

    for b in range(4):
        first(b)
    for q in range(1, NR):
        if q == (2 if own else 1):
            decode(0 if own else 1, 3, [B[1]], [[arrived("rr", 1), got[b]] for b in range(4)])
        if q == B[3]:
            decode(0 if B[0] == q - 1 else 1, 1, [q], [[got[b]] for b in range(4)])
        for b in range(4):
            pick(q, b)
        for b in range(4):
            add(q, b)
    for a, z in YP:
        r = []
        for b in range(4):
            out = T.ys[:, 4 * a + b:4 * z:4]
            src = T.P[:, PW * b:PW * b + PW].indirect(T.oL[:, a // 16:z // 16])
            dep = [got[b], oL]
            r.append(cp(out, src, dep) if b < 2 else act(out, src, F.Copy, dep))
        st = dma("y", "sty", T.y[:, 4 * a:4 * z], T.ys[:, 4 * a:4 * z], r)
    need("y", [(k, n) for k, n in tot.items()] + [("c" + k, n) for k, n in cnt.items()])
